import numpy as np
import ml_dtypes


def mxq(x, axis, fmt="e4m3"):
    dtype, down = {"e4m3": (ml_dtypes.float8_e4m3fn, 7), "e5m2": (ml_dtypes.float8_e5m2, 14)}[fmt]
    v = np.moveaxis(np.asarray(x, np.float32).astype(ml_dtypes.bfloat16).astype(np.float64), axis, -1)
    blocks = v.reshape(v.shape[:-1] + (-1, 32))
    amax = np.abs(blocks).max(-1, keepdims=True)
    byte = np.maximum(np.where(amax > 0, np.frexp(amax)[1] - 1 + 127, 0) - down, 1)
    scale = np.exp2(byte - 127.0)
    codes = (blocks / scale).astype(np.float32).astype(dtype).astype(np.float64)
    return np.moveaxis((codes * scale).reshape(v.shape), -1, axis)


WIDE = False


def mx_kscale(k):
    if not WIDE:
        return np.ones(k)
    levels = np.array([10, -10, 5, -5, 0])
    if k % 512:
        return np.exp2(np.random.permutation(np.resize(levels, k // 32))).repeat(32)
    a = np.empty((k // 512, 16))
    for p in range(k // 512):
        a[p, :8] = np.random.permutation(np.resize(levels, 8))
        for g in range(8):
            far = levels[np.abs(levels - a[p, g]) >= 10]
            a[p, g + 8] = far[np.random.randint(len(far))]
    return np.exp2(a.ravel()).repeat(32)


def f64(x):
    return np.asarray(x).astype(np.float64)


def striped(idx):
    return np.tile(idx.reshape(-1, 16).T, (8, 1)).astype(np.uint16)


def unstriped(offs):
    return offs[:16].T.reshape(-1).astype(np.int64)


def striped8(idx):
    return np.concatenate([x.reshape(-1, 16).T for x in idx]).astype(np.uint16)


def runs(offs, k):
    lists = np.stack([offs[16 * r : 16 * r + 16].T.reshape(-1) for r in range(8)]).astype(np.int64)
    return lists[np.arange(k) % 512 // 64]


def pack_weight(w):
    k, n = w.shape
    w = f64(np.asarray(w, np.float32).astype(ml_dtypes.bfloat16)).reshape(k // 32, 32, n)
    amax = np.abs(w).max(1)
    byte = np.clip(np.where(amax > 0, np.frexp(amax)[1] - 1 + 127 - 7, 1), 1, 254)
    scaled = (w * np.exp2(127.0 - byte)[:, None, :]).reshape(k, n).astype(np.float32)
    words = np.ascontiguousarray(scaled.reshape(k // 512, 128, 4, n).transpose(0, 1, 3, 2)).astype(ml_dtypes.float8_e4m3fn).view(np.uint8)
    return words, np.ascontiguousarray(byte.astype(np.uint8).reshape(k // 512, 16, n))


def unpack_weight(words, scales):
    g, p, n, _ = words.shape
    vals = np.ascontiguousarray(words).view(ml_dtypes.float8_e4m3fn).astype(np.float64) * np.repeat(np.exp2(scales.astype(np.float64) - 127.0), 8, axis=1)[..., None]
    return vals.transpose(0, 1, 3, 2).reshape(g * 512, n)


E2M1 = np.array([0.0, 0.5, 1.0, 1.5, 2.0, 3.0, 4.0, 6.0, -0.0, -0.5, -1.0, -1.5, -2.0, -3.0, -4.0, -6.0])


def pack_fp4(w):
    k, n = w.shape
    w = f64(np.asarray(w, np.float32).astype(ml_dtypes.bfloat16)).reshape(k // 32, 32, n)
    amax = np.abs(w).max(1)
    mant, ex = np.frexp(amax / 6.0)
    byte = np.clip(np.where(amax > 0, np.where(mant > 0.5, ex, ex - 1) + 127, 1), 1, 254)
    scaled = (w * np.exp2(127.0 - byte)[:, None, :]).reshape(k, n).astype(np.float32)
    c = np.ascontiguousarray(scaled.reshape(k // 512, 128, 4, n).transpose(0, 1, 3, 2)).astype(ml_dtypes.float4_e2m1fn).view(np.uint8) & 0xF
    words = (c[..., 0::2] | (c[..., 1::2] << 4)).reshape(k // 512, 128, 2 * n)
    return np.ascontiguousarray(words), np.ascontiguousarray(byte.astype(np.uint8).reshape(k // 512, 16, n))


def unpack_fp4(words, scales):
    g, _, n = scales.shape
    words = np.ascontiguousarray(words).reshape(g, 128, n, 2)
    nib = np.empty((g, 128, n, 4), np.uint8)
    nib[..., 0::2] = words & 0xF
    nib[..., 1::2] = words >> 4
    vals = E2M1[nib] * np.repeat(np.exp2(scales.astype(np.float64) - 127.0), 8, axis=1)[..., None]
    return vals.transpose(0, 1, 3, 2).reshape(g * 512, n)


def planes(y):
    n, m = y.shape
    v = y.astype(np.float32).astype(ml_dtypes.bfloat16).astype(np.float64).reshape(n // 32, 32, m)
    top = np.abs(v).max(1)
    byte = np.clip(np.where(top > 0, np.frexp(top)[1] - 1 + 127 - 7, 1), 1, 254)
    codes = (v * np.exp2(127.0 - byte)[:, None, :]).reshape(n, m).astype(np.float32).astype(ml_dtypes.float8_e4m3fn).view(np.uint8)
    words = codes.reshape(n // 512, 128, 4, m).transpose(0, 1, 3, 2)
    return np.ascontiguousarray(words), np.ascontiguousarray(byte.astype(np.uint8).reshape(n // 512, 16, m))


K, T, S, V, H = 512, 2048, 512, 512, 512


def setup_inputs():
    n = np.random.standard_normal
    s = mx_kscale(K)[:, None]
    u = mx_kscale(S)
    packed_xT = pack_weight(n((K, T)) * s)
    packed_w1 = pack_fp4(n((K, H)) / np.sqrt(K) / s)
    packed_w2 = pack_fp4(n((K, H)) / np.sqrt(K) / s)
    packed_w3 = pack_fp4(n((K, H)) / np.sqrt(K) / s)
    return {
        "x_words": packed_xT[0],
        "x_scales": packed_xT[1],
        "w1_words": packed_w1[0],
        "w1_scales": packed_w1[1],
        "w2_words": packed_w2[0],
        "w2_scales": packed_w2[1],
        "w3_words": packed_w3[0],
        "w3_scales": packed_w3[1],
        "ga": (np.random.uniform(0.5, 1.5, (H, 1)) * u[:, None]).astype(np.float32),
        "gb": (np.random.uniform(0.5, 1.5, (H, 1)) / u[:, None]).astype(np.float32),
        "offs": striped(np.random.permutation(T)[:S]),
        "two": striped(np.random.permutation(T)[:S]),
        "n1": striped8(np.stack([np.random.permutation(S) for _ in range(8)])),
        "n2": striped8(np.stack([np.random.permutation(S) for _ in range(8)])),
        "three": striped(np.random.permutation(T)[:V]),
        "n3": striped8(np.stack([np.random.permutation(V) for _ in range(8)])),
        "n4": striped8(np.stack([np.random.permutation(V) for _ in range(8)])),
        "n5": striped8(np.stack([np.random.permutation(V) for _ in range(8)])),
        "n6": striped8(np.stack([np.random.permutation(V) for _ in range(8)])),
    }


def reference(x_words, x_scales, w1_words, w1_scales, w2_words, w2_scales, w3_words, w3_scales, ga, gb, offs, two, n1, n2, three, n3, n4, n5, n6):
    xq = unpack_weight(x_words, x_scales)[:, unstriped(offs)]
    y = unpack_fp4(w1_words, w1_scales).T @ xq
    x_two = unpack_weight(x_words, x_scales)[:, unstriped(two)]
    d = unpack_fp4(w2_words, w2_scales).T @ x_two
    z = f64(ga) * (0.75 * (y * (d[np.arange(H)[:, None], runs(n2, H)]) - ((y[np.arange(H)[:, None], runs(n1, H)]) * d)))
    x_three = unpack_weight(x_words, x_scales)[:, unstriped(three)]
    b = unpack_fp4(w3_words, w3_scales).T @ x_three
    pa = b[np.arange(H)[:, None], runs(n3, H)]
    pb = b[np.arange(H)[:, None], runs(n4, H)]
    z2 = f64(gb) * (np.maximum(np.minimum(b, pa), np.minimum(np.maximum(b, pa), pb)))
    s = 0.0625 * ((mxq(z, 0, "e4m3").T @ mxq(z2, 0, "e4m3")))
    out_0 = np.minimum(np.maximum(s, s[np.arange(S)[:, None], runs(n5, S)]), s[np.arange(S)[:, None], runs(n6, S)])
    return (out_0,) + planes(out_0)

@@ -1,0 +1,277 @@
+from contextlib import ExitStack
+
+import concourse.mybir as mybir
+from concourse.masks import make_identity
+
+F32 = mybir.dt.float32
+BF16 = mybir.dt.bfloat16
+I32 = mybir.dt.int32
+U32 = mybir.dt.uint32
+U16 = mybir.dt.uint16
+U8 = mybir.dt.uint8
+FP8X4 = mybir.dt.float8_e4m3fn_x4
+FP4X4 = mybir.dt.float4_e2m1fn_x4
+ALU = mybir.AluOpType
+COPY = mybir.ActivationFunctionType.Copy
+
+P = 128
+T = 2048
+N = 512
+HALF = 256
+FLOPS = 4 * 2 * 512 * 512 * 512
+
+
+def tile_picked_twkcrossbmedminmx_none_po_kernel(
+    tc, x_words, x_scales, w1_words, w1_scales, w2_words, w2_scales, w3_words, w3_scales,
+    ga, gb, offs, two, n1, n2, three, n3, n4, n5, n6, out_0, out_1, out_2,
+):
+    nc = tc.nc
+    with ExitStack() as ctx:
+        keep = ctx.enter_context(tc.tile_pool(name="keep", bufs=1))
+        held = ctx.enter_context(tc.psum_pool(name="held", bufs=4))
+        ring = ctx.enter_context(tc.psum_pool(name="ring", bufs=4))
+
+        def sb(name, shape, dtype):
+            return keep.tile(shape, dtype, name=name, align_bytes=64)
+
+        lists = {}
+
+        def load_list(name, src):
+            lists[name] = keep.tile([P, N // 16], U16, name="list_" + name)
+            nc.sync.dma_start(lists[name][:], src)
+
+        def load_scale_rows(queue, tile, src):
+            rows = src[0].bitcast(I32)
+            for q in range(4):
+                queue.dma_start(tile[32 * q : 32 * q + 4, :].bitcast(I32), rows[4 * q : 4 * q + 4, :])
+
+        xs = sb("xs", [P, T], U8)
+        nc.vector.memset(xs[:].bitcast(I32), 0)
+        w_raw_s = [sb("wrs%d" % i, [P, N], U8) for i in range(3)]
+        nc.vector.memset(w_raw_s[0][:].bitcast(I32), 0)
+        g_rows = sb("g_rows", [P, P], F32)
+        nc.vector.memset(g_rows[:], 0.0)
+        for i in (1, 2):
+            nc.vector.memset(w_raw_s[i][:].bitcast(I32), 0)
+        ident = sb("ident", [P, P], F32)
+        make_identity(nc, ident[:])
+
+        xw = sb("xw", [P, T], I32)
+        nc.sync.dma_start(xw[:], x_words[0].rearrange("p n t -> p (n t)").bitcast(I32))
+        load_list("offs", offs)
+        load_scale_rows(nc.sync, xs, x_scales)
+        load_list("two", two)
+        w_raw = [sb("wr%d" % i, [P, 2 * N], U8) for i in range(3)]
+        nc.sync.dma_start(w_raw[0][:].bitcast(I32), w1_words[0].bitcast(I32))
+        nc.scalar.dma_start(w_raw[2][:].bitcast(I32), w3_words[0].bitcast(I32))
+        load_list("three", three)
+        load_scale_rows(nc.sync, w_raw_s[0], w1_scales)
+        for i, g in enumerate((ga, gb)):
+            nc.sync.dma_start(
+                g_rows[4 * i : 4 * i + 4, :].rearrange("t (q r) -> t q r", r=8),
+                g.rearrange("(q t r) o -> t q (r o)", t=4, r=8),
+            )
+        nc.sync.dma_start(w_raw[1][:].bitcast(I32), w2_words[0].bitcast(I32))
+        load_scale_rows(nc.gpsimd, w_raw_s[1], w2_scales)
+        load_scale_rows(nc.gpsimd, w_raw_s[2], w3_scales)
+        for name, src in (("n2", n2), ("n1", n1), ("n3", n3), ("n4", n4), ("n5", n5), ("n6", n6)):
+            load_list(name, src)
+
+        g_ps = ring.tile([P, P], F32, name="ring")
+        nc.tensor.transpose(g_ps[:], g_rows[:], ident[:])
+        gains = sb("gains", [P, 8], F32)
+        nc.scalar.activation(gains[:], g_ps[:, 0:8], COPY)
+
+        picked = {}
+
+        def pick(name):
+            words = sb("pw_" + name, [P, N], U32)
+            scales = sb("ps_" + name, [P, N], U8)
+            nc.vector.tensor_copy(scales[:], xs[:].indirect(lists[name][:]))
+            nc.vector.tensor_copy(words[:], xw[:].bitcast(U32).indirect(lists[name][:]))
+            picked[name] = (words, scales)
+
+        dealt = {}
+
+        def deal(i):
+            words = sb("wd%d" % i, [P, 2 * N], U8)
+            scales = sb("wds%d" % i, [P, N], U8)
+            nc.vector.tensor_copy(
+                words[:].bitcast(I32).rearrange("p (t q e) -> p t q e", t=4, e=4),
+                w_raw[i][:].bitcast(I32).rearrange("p (q t e) -> p t q e", t=4, e=4),
+            )
+            nc.vector.tensor_copy(
+                scales[:].bitcast(I32).rearrange("p (t q e) -> p t q e", t=4, e=2),
+                w_raw_s[i][:].bitcast(I32).rearrange("p (q t e) -> p t q e", t=4, e=2),
+            )
+            dealt[i] = (words, scales)
+
+        def project(i, name, t):
+            acc = ring.tile([P, N], F32, name="ring")
+            nc.tensor.matmul_mx(
+                out=acc[:],
+                lhsT=dealt[i][0][:, 2 * P * t : 2 * P * (t + 1)].bitcast(FP4X4),
+                lhsT_scale=dealt[i][1][:, P * t : P * (t + 1)],
+                rhs=picked[name][0][:].bitcast(FP8X4),
+                rhs_scale=picked[name][1][:],
+                start=True,
+                stop=True,
+            )
+            return acc
+
+        pick("offs")
+        deal(0)
+        pick("two")
+        deal(1)
+        pick("three")
+        deal(2)
+
+        ys = [sb("ys%d" % t, [P, N], F32) for t in range(4)]
+        dd = [sb("dd%d" % t, [P, 2 * N], F32) for t in range(4)]
+        for t in range(4):
+            acc = project(0, "offs", t)
+            nc.scalar.activation(ys[t][:], acc[:], COPY, scale=gains[:, t : t + 1])
+        for t in range(4):
+            acc = project(1, "two", t)
+            nc.scalar.activation(dd[t][:, 0:N], acc[:], COPY, scale=0.75)
+            nc.scalar.activation(dd[t][:, N : 2 * N], acc[:], COPY, scale=-0.75)
+        bw = [sb("bw%d" % t, [P, N], F32) for t in range(4)]
+        bp = sb("bp", [P, 4, N], F32)
+        for t in range(4):
+            acc = project(2, "three", t)
+            nc.scalar.activation(bw[t][:], acc[:], COPY, scale=gains[:, 4 + t : 5 + t])
+            nc.scalar.activation(bp[:, t, :], acc[:], COPY, scale=gains[:, 4 + t : 5 + t])
+
+        def add_turned(bank, t, first, second):
+            nc.tensor.matmul(bank[:, t, :], first, ident[:], start=True, stop=False, is_transpose=True)
+            nc.tensor.matmul(bank[:, t, :], second, ident[:], start=False, stop=True, is_transpose=True)
+
+        def round_turned(name, bank):
+            pairs = sb(name, [P, 2, P, 2], BF16)
+            nc.scalar.copy(pairs[:], bank[:].rearrange("j (u e) p -> j u p e", e=2))
+            return pairs[:].rearrange("j u p e -> j (u p e)").bitcast(F32)
+
+        z_banks = [held.tile([P, 4, P], F32, name="held") for b in range(4)]
+        for t in range(4):
+            p1 = sb("p1_%d" % t, [P, N], F32)
+            p2 = sb("p2_%d" % t, [P, N], F32)
+            nc.vector.tensor_tensor(p1[:], dd[t][:].indirect(lists["n2"][:]), ys[t][:], ALU.mult)
+            for h in range(2):
+                nc.vector.tensor_tensor(
+                    p2[:, HALF * h : HALF * (h + 1)],
+                    ys[t][:].indirect(lists["n1"][:, 16 * h : 16 * (h + 1)]),
+                    dd[t][:, N + HALF * h : N + HALF * (h + 1)],
+                    ALU.mult,
+                )
+            for b in range(4):
+                cols = slice(P * b, P * (b + 1))
+                add_turned(z_banks[b], t, p1[:, cols], p2[:, cols])
+
+        z_in = sb("z_in", [P, N * 4], BF16)
+        z_in_words = z_in[:].bitcast(F32).rearrange("p (t m u) -> p t m u", t=4, u=2)
+        for k in range(2):
+            back = ring.tile([P, 2, 2 * P], F32, name="ring")
+            for c in range(2):
+                words = round_turned("zt%d" % (2 * k + c), z_banks[2 * k + c])
+                for u in range(2):
+                    nc.tensor.transpose(back[:, u, P * c : P * (c + 1)], words[:, P * u : P * (u + 1)], ident[:])
+            nc.scalar.copy(z_in_words[:, :, 64 * k : 64 * (k + 1), :], back[:].rearrange("p u (m t) -> p t m u", t=4))
+        z_words = sb("z_words", [P, N], U32)
+        z_scales = sb("z_scales", [P, N], U8)
+
+        r = [sb("r%d" % h, [P, 4, HALF], F32) for h in range(2)]
+
+        def median_step(t, h):
+            cols = slice(HALF * h, HALF * (h + 1))
+            u = sb("u%d_%d" % (t, h), [P, HALF], F32)
+            v = sb("v%d_%d" % (t, h), [P, HALF], F32)
+            m = sb("m%d_%d" % (t, h), [P, HALF], F32)
+            nc.vector.tensor_tensor(u[:], bw[t][:].indirect(lists["n3"][:, 16 * h : 16 * (h + 1)]), bp[:, t, cols], ALU.subtract)
+            nc.vector.tensor_tensor(v[:], bw[t][:].indirect(lists["n4"][:, 16 * h : 16 * (h + 1)]), bp[:, t, cols], ALU.subtract)
+            nc.vector.scalar_tensor_tensor(m[:], u[:], 0.0, v[:], ALU.max, ALU.min)
+            nc.vector.scalar_tensor_tensor(r[h][:, t, :], u[:], 0.0, m[:], ALU.min, ALU.max)
+
+        z2_words = sb("z2_words", [P, N], U32)
+        z2_scales = sb("z2_scales", [P, N], U8)
+
+        z2_banks = [ring.tile([P, 4, P], F32, name="ring") for b in range(2)]
+        for t in range(4):
+            median_step(t, 0)
+            for b in range(2):
+                add_turned(z2_banks[b], t, r[0][:, t, P * b : P * (b + 1)], bp[:, t, P * b : P * (b + 1)])
+        nc.vector.quantize_mx(out=z_words[:].bitcast(FP8X4), scales=z_scales[:], in_=z_in[:])
+        back = ring.tile([P, 2, HALF], F32, name="ring")
+        for c in range(2):
+            words = round_turned("z2t%d" % c, z2_banks[c])
+            for u in range(2):
+                nc.tensor.transpose(back[:, u, P * c : P * (c + 1)], words[:, P * u : P * (u + 1)], ident[:])
+        z2_in0 = sb("z2_in0", [P, HALF * 4], BF16)
+        nc.scalar.copy(z2_in0[:].bitcast(F32).rearrange("p (c u) -> p c u", u=2), back[:].rearrange("p u c -> p c u"))
+
+        for t in range(4):
+            median_step(t, 1)
+        nc.vector.quantize_mx(out=z2_words[:, 0:HALF].bitcast(FP8X4), scales=z2_scales[:, 0:HALF], in_=z2_in0[:])
+
+        s_banks = [held.tile([P, N], F32, name="held") for t in range(4)]
+        sw = [sb("sw%d" % t, [P, N], F32) for t in range(4)]
+
+        def score(t, h):
+            cols = slice(HALF * h, HALF * (h + 1))
+            nc.tensor.matmul_mx(
+                out=s_banks[t][:, cols],
+                lhsT=z_words[:, P * t : P * (t + 1)].bitcast(FP8X4),
+                lhsT_scale=z_scales[:, P * t : P * (t + 1)],
+                rhs=z2_words[:, cols].bitcast(FP8X4),
+                rhs_scale=z2_scales[:, cols],
+                start=True,
+                stop=True,
+            )
+            nc.scalar.activation(sw[t][:, cols], s_banks[t][:, cols], COPY, scale=0.0625)
+
+        for t in range(4):
+            score(t, 0)
+
+        z2_in1 = [sb("z2_in1_%d" % c, [P, P * 4], BF16) for c in range(2)]
+        for c in range(2):
+            nc.vector.tensor_tensor(
+                z2_in1[c][:].rearrange("p (c i t) -> p c t i", i=2, t=4),
+                r[1][:, :, P * c : P * (c + 1)].rearrange("p t (c i) -> p c t i", i=2),
+                bp[:, :, HALF + P * c : HALF + P * (c + 1)].rearrange("p t (c i) -> p c t i", i=2),
+                ALU.add,
+            )
+        for c in range(2):
+            cols = slice(HALF + P * c, HALF + P * (c + 1))
+            nc.vector.quantize_mx(out=z2_words[:, cols].bitcast(FP8X4), scales=z2_scales[:, cols], in_=z2_in1[c][:])
+        for t in range(4):
+            score(t, 1)
+
+        o_words = sb("o_words", [P, N], U32)
+        o_scales = sb("o_scales", [P, N], U8)
+        out_rows = out_0.rearrange("(p t) v -> p t v", t=4)
+        out_words = out_1[0].rearrange("p n t -> p (n t)").bitcast(I32)
+        chunks = ((0, 256), (256, 384), (384, 512))
+        for ci, (c0, c1) in enumerate(chunks):
+            width = c1 - c0
+            o = sb("o%d" % ci, [P, 4, width], F32)
+            for t in range(4):
+                g5 = sb("g5_%d_%d" % (ci, t), [P, width], F32)
+                g6 = sb("g6_%d_%d" % (ci, t), [P, width], F32)
+                top = sb("top%d_%d" % (ci, t), [P, width], F32)
+                nc.vector.tensor_copy(g5[:], sw[t][:].indirect(lists["n5"][:, c0 // 16 : c1 // 16]))
+                nc.vector.tensor_copy(g6[:], sw[t][:].indirect(lists["n6"][:, c0 // 16 : c1 // 16]))
+                nc.vector.tensor_tensor(top[:], g5[:], sw[t][:, c0:c1], ALU.max)
+                nc.vector.tensor_tensor(o[:, t, :], top[:], g6[:], ALU.min)
+            nc.sync.dma_start(out_rows[:, :, c0:c1], o[:])
+            o_in = sb("o_in%d" % ci, [P, width * 4], BF16)
+            dst = o_in[:].rearrange("p (c i t) -> p c t i", i=4, t=4)
+            src = o[:].rearrange("p t (c i) -> p c t i", i=4)
+            if ci == len(chunks) - 1:
+                nc.vector.tensor_copy(dst, src)
+            else:
+                nc.scalar.copy(dst, src)
+            nc.vector.quantize_mx(out=o_words[:, c0:c1].bitcast(FP8X4), scales=o_scales[:, c0:c1], in_=o_in[:])
+            nc.sync.dma_start(out_words[:, c0:c1], o_words[:, c0:c1].bitcast(I32))
+        scale_rows = out_2[0].bitcast(I32)
+        for q in range(4):
+            queue = nc.sync if q % 2 else nc.scalar
+            queue.dma_start(scale_rows[4 * q : 4 * q + 4, :], o_scales[32 * q : 32 * q + 4, :].bitcast(I32))

@@ -28,11 +28,11 @@ def tile_picked_twkcrossbmedminmx_none_po_kernel(
     nc = tc.nc
     with ExitStack() as ctx:
         keep = ctx.enter_context(tc.tile_pool(name="keep", bufs=1))
-        held = ctx.enter_context(tc.psum_pool(name="held", bufs=4))
         ring = ctx.enter_context(tc.psum_pool(name="ring", bufs=4))
+        held = ctx.enter_context(tc.psum_pool(name="held", bufs=1))
 
-        def sb(name, shape, dtype):
-            return keep.tile(shape, dtype, name=name, align_bytes=64)
+        def sb(name, shape, dtype, tag=None):
+            return keep.tile(shape, dtype, name=name, tag=tag or name, align_bytes=64)
 
         lists = {}
 
@@ -46,25 +46,23 @@ def tile_picked_twkcrossbmedminmx_none_po_kernel(
                 queue.dma_start(tile[32 * q : 32 * q + 4, :].bitcast(I32), rows[4 * q : 4 * q + 4, :])
 
         xs = sb("xs", [P, T], U8)
-        nc.vector.memset(xs[:].bitcast(I32), 0)
+        nc.gpsimd.memset(xs[:].bitcast(I32), 0)
         w_raw_s = [sb("wrs%d" % i, [P, N], U8) for i in range(3)]
-        nc.vector.memset(w_raw_s[0][:].bitcast(I32), 0)
+        nc.gpsimd.memset(w_raw_s[0][:].bitcast(I32), 0)
         g_rows = sb("g_rows", [P, P], F32)
-        nc.vector.memset(g_rows[:], 0.0)
+        nc.gpsimd.memset(g_rows[:], 0.0)
         for i in (1, 2):
-            nc.vector.memset(w_raw_s[i][:].bitcast(I32), 0)
+            nc.gpsimd.memset(w_raw_s[i][:].bitcast(I32), 0)
         ident = sb("ident", [P, P], F32)
         make_identity(nc, ident[:])
 
         xw = sb("xw", [P, T], I32)
-        nc.sync.dma_start(xw[:], x_words[0].rearrange("p n t -> p (n t)").bitcast(I32))
+        w_raw = [sb("wr%d" % i, [P, 2 * N], U8) for i in range(3)]
         load_list("offs", offs)
         load_scale_rows(nc.sync, xs, x_scales)
         load_list("two", two)
-        w_raw = [sb("wr%d" % i, [P, 2 * N], U8) for i in range(3)]
+        nc.sync.dma_start(xw[:], x_words[0].rearrange("p n t -> p (n t)").bitcast(I32))
         nc.sync.dma_start(w_raw[0][:].bitcast(I32), w1_words[0].bitcast(I32))
-        nc.scalar.dma_start(w_raw[2][:].bitcast(I32), w3_words[0].bitcast(I32))
-        load_list("three", three)
         load_scale_rows(nc.sync, w_raw_s[0], w1_scales)
         for i, g in enumerate((ga, gb)):
             nc.sync.dma_start(
@@ -72,23 +70,29 @@ def tile_picked_twkcrossbmedminmx_none_po_kernel(
                 g.rearrange("(q t r) o -> t q (r o)", t=4, r=8),
             )
         nc.sync.dma_start(w_raw[1][:].bitcast(I32), w2_words[0].bitcast(I32))
-        load_scale_rows(nc.gpsimd, w_raw_s[1], w2_scales)
-        load_scale_rows(nc.gpsimd, w_raw_s[2], w3_scales)
-        for name, src in (("n2", n2), ("n1", n1), ("n3", n3), ("n4", n4), ("n5", n5), ("n6", n6)):
+        load_scale_rows(nc.sync, w_raw_s[1], w2_scales)
+        load_list("three", three)
+        load_list("n2", n2)
+        load_list("n1", n1)
+        nc.sync.dma_start(w_raw[2][:].bitcast(I32), w3_words[0].bitcast(I32))
+        load_scale_rows(nc.sync, w_raw_s[2], w3_scales)
+        for name, src in (("n3", n3), ("n4", n4), ("n5", n5), ("n6", n6)):
             load_list(name, src)
 
         g_ps = ring.tile([P, P], F32, name="ring")
         nc.tensor.transpose(g_ps[:], g_rows[:], ident[:])
         gains = sb("gains", [P, 8], F32)
         nc.scalar.activation(gains[:], g_ps[:, 0:8], COPY)
+        minus_ga = sb("minus_ga", [P, 4], F32)
+        nc.scalar.activation(minus_ga[:], g_ps[:, 0:4], COPY, scale=-1.0)
 
         picked = {}
 
-        def pick(name):
-            words = sb("pw_" + name, [P, N], U32)
-            scales = sb("ps_" + name, [P, N], U8)
-            nc.vector.tensor_copy(scales[:], xs[:].indirect(lists[name][:]))
+        def pick(name, words_tag=None, scales_tag=None):
+            words = sb("pw_" + name, [P, N], U32, words_tag)
+            scales = sb("ps_" + name, [P, N], U8, scales_tag)
             nc.vector.tensor_copy(words[:], xw[:].bitcast(U32).indirect(lists[name][:]))
+            nc.vector.tensor_copy(scales[:], xs[:].indirect(lists[name][:]))
             picked[name] = (words, scales)
 
         dealt = {}
@@ -106,8 +110,7 @@ def tile_picked_twkcrossbmedminmx_none_po_kernel(
             )
             dealt[i] = (words, scales)
 
-        def project(i, name, t):
-            acc = ring.tile([P, N], F32, name="ring")
+        def project(i, name, t, acc):
             nc.tensor.matmul_mx(
                 out=acc[:],
                 lhsT=dealt[i][0][:, 2 * P * t : 2 * P * (t + 1)].bitcast(FP4X4),
@@ -121,25 +124,24 @@ def tile_picked_twkcrossbmedminmx_none_po_kernel(
 
         pick("offs")
         deal(0)
-        pick("two")
+        pick("two", words_tag="wr0")
         deal(1)
-        pick("three")
+        pick("three", words_tag="wr1", scales_tag="wrs1")
         deal(2)
 
-        ys = [sb("ys%d" % t, [P, N], F32) for t in range(4)]
+        ys = [sb("ys%d" % t, [P, 2 * N], F32) for t in range(4)]
         dd = [sb("dd%d" % t, [P, 2 * N], F32) for t in range(4)]
         for t in range(4):
-            acc = project(0, "offs", t)
-            nc.scalar.activation(ys[t][:], acc[:], COPY, scale=gains[:, t : t + 1])
-        for t in range(4):
-            acc = project(1, "two", t)
+            acc = project(0, "offs", t, ring.tile([P, N], F32, name="ring"))
+            nc.scalar.activation(ys[t][:, 0:N], acc[:], COPY, scale=minus_ga[:, t : t + 1])
+            nc.scalar.activation(ys[t][:, N : 2 * N], acc[:], COPY, scale=gains[:, t : t + 1])
+            acc = project(1, "two", t, ring.tile([P, N], F32, name="ring"))
             nc.scalar.activation(dd[t][:, 0:N], acc[:], COPY, scale=0.75)
-            nc.scalar.activation(dd[t][:, N : 2 * N], acc[:], COPY, scale=-0.75)
-        bw = [sb("bw%d" % t, [P, N], F32) for t in range(4)]
-        bp = sb("bp", [P, 4, N], F32)
+        bw = [sb("bw%d" % t, [P, 2 * N], F32) for t in range(4)]
+        bp = sb("bp", [P, 4, N], BF16)
         for t in range(4):
-            acc = project(2, "three", t)
-            nc.scalar.activation(bw[t][:], acc[:], COPY, scale=gains[:, 4 + t : 5 + t])
+            acc = project(2, "three", t, held.tile([P, N], F32, name="held%d" % t))
+            nc.scalar.activation(bw[t][:, 0:N], acc[:], COPY, scale=gains[:, 4 + t : 5 + t])
             nc.scalar.activation(bp[:, t, :], acc[:], COPY, scale=gains[:, 4 + t : 5 + t])
 
         def add_turned(bank, t, first, second):
@@ -151,18 +153,12 @@ def tile_picked_twkcrossbmedminmx_none_po_kernel(
             nc.scalar.copy(pairs[:], bank[:].rearrange("j (u e) p -> j u p e", e=2))
             return pairs[:].rearrange("j u p e -> j (u p e)").bitcast(F32)
 
-        z_banks = [held.tile([P, 4, P], F32, name="held") for b in range(4)]
+        z_banks = [held.tile([P, 4, P], F32, name="held%d" % b) for b in range(4)]
         for t in range(4):
             p1 = sb("p1_%d" % t, [P, N], F32)
             p2 = sb("p2_%d" % t, [P, N], F32)
-            nc.vector.tensor_tensor(p1[:], dd[t][:].indirect(lists["n2"][:]), ys[t][:], ALU.mult)
-            for h in range(2):
-                nc.vector.tensor_tensor(
-                    p2[:, HALF * h : HALF * (h + 1)],
-                    ys[t][:].indirect(lists["n1"][:, 16 * h : 16 * (h + 1)]),
-                    dd[t][:, N + HALF * h : N + HALF * (h + 1)],
-                    ALU.mult,
-                )
+            nc.vector.tensor_tensor(p1[:], dd[t][:].indirect(lists["n2"][:]), ys[t][:, N : 2 * N], ALU.mult)
+            nc.vector.tensor_tensor(p2[:], ys[t][:].indirect(lists["n1"][:]), dd[t][:, 0:N], ALU.mult)
             for b in range(4):
                 cols = slice(P * b, P * (b + 1))
                 add_turned(z_banks[b], t, p1[:, cols], p2[:, cols])
@@ -176,101 +172,120 @@ def tile_picked_twkcrossbmedminmx_none_po_kernel(
                 for u in range(2):
                     nc.tensor.transpose(back[:, u, P * c : P * (c + 1)], words[:, P * u : P * (u + 1)], ident[:])
             nc.scalar.copy(z_in_words[:, :, 64 * k : 64 * (k + 1), :], back[:].rearrange("p u (m t) -> p t m u", t=4))
-        z_words = sb("z_words", [P, N], U32)
-        z_scales = sb("z_scales", [P, N], U8)
 
-        r = [sb("r%d" % h, [P, 4, HALF], F32) for h in range(2)]
+        pa = sb("pa", [P, 4, N], BF16)
+        pb = sb("pb", [P, 4, N], BF16)
+        lo = sb("lo", [P, 4, N], BF16)
+        hi = sb("hi", [P, 4, N], BF16)
+        mid = sb("mid", [P, 4, N], BF16)
+        for t in range(4):
+            nc.vector.tensor_copy(pa[:, t, :], bw[t][:].indirect(lists["n3"][:]))
+            nc.vector.tensor_copy(pb[:, t, :], bw[t][:].indirect(lists["n4"][:]))
+        z_codes = []
 
-        def median_step(t, h):
-            cols = slice(HALF * h, HALF * (h + 1))
-            u = sb("u%d_%d" % (t, h), [P, HALF], F32)
-            v = sb("v%d_%d" % (t, h), [P, HALF], F32)
-            m = sb("m%d_%d" % (t, h), [P, HALF], F32)
-            nc.vector.tensor_tensor(u[:], bw[t][:].indirect(lists["n3"][:, 16 * h : 16 * (h + 1)]), bp[:, t, cols], ALU.subtract)
-            nc.vector.tensor_tensor(v[:], bw[t][:].indirect(lists["n4"][:, 16 * h : 16 * (h + 1)]), bp[:, t, cols], ALU.subtract)
-            nc.vector.scalar_tensor_tensor(m[:], u[:], 0.0, v[:], ALU.max, ALU.min)
-            nc.vector.scalar_tensor_tensor(r[h][:, t, :], u[:], 0.0, m[:], ALU.min, ALU.max)
+        def quantize_z(t, tag):
+            words = sb("z_words%d" % t, [P, P], U32, tag)
+            scales = sb("z_scales%d" % t, [P, P], U8)
+            nc.vector.quantize_mx(out=words[:].bitcast(FP8X4), scales=scales[:], in_=z_in[:, N * t : N * (t + 1)])
+            z_codes.append((words, scales))
+
+        quantize_z(0, None)
+        nc.vector.tensor_tensor(lo[:, 0:2, :], pa[:, 0:2, :], pb[:, 0:2, :], ALU.min)
+        nc.vector.tensor_tensor(lo[:, 2:4, :], pa[:, 2:4, :], pb[:, 2:4, :], ALU.min)
+        nc.vector.tensor_tensor(hi[:], pa[:], pb[:], ALU.max)
+        nc.vector.tensor_tensor(mid[:, 0:2, :], lo[:, 0:2, :], bp[:, 0:2, :], ALU.max)
+        nc.vector.tensor_tensor(mid[:, 2:4, :], lo[:, 2:4, :], bp[:, 2:4, :], ALU.max)
 
         z2_words = sb("z2_words", [P, N], U32)
         z2_scales = sb("z2_scales", [P, N], U8)
-
-        z2_banks = [ring.tile([P, 4, P], F32, name="ring") for b in range(2)]
-        for t in range(4):
-            median_step(t, 0)
-            for b in range(2):
-                add_turned(z2_banks[b], t, r[0][:, t, P * b : P * (b + 1)], bp[:, t, P * b : P * (b + 1)])
-        nc.vector.quantize_mx(out=z_words[:].bitcast(FP8X4), scales=z_scales[:], in_=z_in[:])
-        back = ring.tile([P, 2, HALF], F32, name="ring")
+        z2_in = [sb("z2_in%d" % h, [P, HALF * 4], BF16) for h in range(2)]
         for c in range(2):
-            words = round_turned("z2t%d" % c, z2_banks[c])
-            for u in range(2):
-                nc.tensor.transpose(back[:, u, P * c : P * (c + 1)], words[:, P * u : P * (u + 1)], ident[:])
-        z2_in0 = sb("z2_in0", [P, HALF * 4], BF16)
-        nc.scalar.copy(z2_in0[:].bitcast(F32).rearrange("p (c u) -> p c u", u=2), back[:].rearrange("p u c -> p c u"))
-
-        for t in range(4):
-            median_step(t, 1)
-        nc.vector.quantize_mx(out=z2_words[:, 0:HALF].bitcast(FP8X4), scales=z2_scales[:, 0:HALF], in_=z2_in0[:])
-
-        s_banks = [held.tile([P, N], F32, name="held") for t in range(4)]
-        sw = [sb("sw%d" % t, [P, N], F32) for t in range(4)]
-
-        def score(t, h):
+            cols = slice(P * c, P * (c + 1))
+            flat = sb("z2_flat%d" % c, [P, 4, P], BF16)
+            nc.vector.tensor_tensor(flat[:], mid[:, :, cols], hi[:, :, cols], ALU.min)
+            nc.scalar.copy(
+                z2_in[0][:, N * c : N * (c + 1)].rearrange("p (c i t) -> p c t i", i=4, t=4),
+                flat[:].rearrange("p t (c i) -> p c t i", i=4),
+            )
+        nc.vector.tensor_tensor(
+            z2_in[1][:].rearrange("p (c i t) -> p c t i", i=4, t=4),
+            mid[:, :, HALF:N].rearrange("p t (c i) -> p c t i", i=4),
+            hi[:, :, HALF:N].rearrange("p t (c i) -> p c t i", i=4),
+            ALU.min,
+        )
+        for h in range(2):
             cols = slice(HALF * h, HALF * (h + 1))
+            nc.vector.quantize_mx(out=z2_words[:, cols].bitcast(FP8X4), scales=z2_scales[:, cols], in_=z2_in[h][:])
+        for t, tag in ((1, "z2_in0"), (2, "mid"), (3, "hi")):
+            quantize_z(t, tag)
+
+        sw = [sb("sw%d" % t, [P, N], F32) for t in range(4)]
+        sp = sb("sp", [P, 4, N], F32)
+        s_banks = [held.tile([P, N], F32, name="held%d" % t) for t in range(4)]
+
+        def score(t, c0, c1):
             nc.tensor.matmul_mx(
-                out=s_banks[t][:, cols],
-                lhsT=z_words[:, P * t : P * (t + 1)].bitcast(FP8X4),
-                lhsT_scale=z_scales[:, P * t : P * (t + 1)],
-                rhs=z2_words[:, cols].bitcast(FP8X4),
-                rhs_scale=z2_scales[:, cols],
+                out=s_banks[t][:, c0:c1],
+                lhsT=z_codes[t][0][:].bitcast(FP8X4),
+                lhsT_scale=z_codes[t][1][:],
+                rhs=z2_words[:, c0:c1].bitcast(FP8X4),
+                rhs_scale=z2_scales[:, c0:c1],
                 start=True,
                 stop=True,
             )
-            nc.scalar.activation(sw[t][:, cols], s_banks[t][:, cols], COPY, scale=0.0625)
+            nc.scalar.activation(sw[t][:, c0:c1], s_banks[t][:, c0:c1], COPY, scale=0.0625)
 
-        for t in range(4):
-            score(t, 0)
-
-        z2_in1 = [sb("z2_in1_%d" % c, [P, P * 4], BF16) for c in range(2)]
-        for c in range(2):
-            nc.vector.tensor_tensor(
-                z2_in1[c][:].rearrange("p (c i t) -> p c t i", i=2, t=4),
-                r[1][:, :, P * c : P * (c + 1)].rearrange("p t (c i) -> p c t i", i=2),
-                bp[:, :, HALF + P * c : HALF + P * (c + 1)].rearrange("p t (c i) -> p c t i", i=2),
-                ALU.add,
-            )
-        for c in range(2):
-            cols = slice(HALF + P * c, HALF + P * (c + 1))
-            nc.vector.quantize_mx(out=z2_words[:, cols].bitcast(FP8X4), scales=z2_scales[:, cols], in_=z2_in1[c][:])
-        for t in range(4):
-            score(t, 1)
+        score(0, 0, HALF)
+        score(0, HALF, N)
+        for t in range(1, 4):
+            score(t, 0, N)
+        for h in range(2):
+            for t in range(4):
+                cols = slice(HALF * h, HALF * (h + 1))
+                nc.scalar.activation(sp[:, t, cols], s_banks[t][:, cols], COPY, scale=0.0625)
 
         o_words = sb("o_words", [P, N], U32)
         o_scales = sb("o_scales", [P, N], U8)
         out_rows = out_0.rearrange("(p t) v -> p t v", t=4)
         out_words = out_1[0].rearrange("p n t -> p (n t)").bitcast(I32)
-        chunks = ((0, 256), (256, 384), (384, 512))
-        for ci, (c0, c1) in enumerate(chunks):
-            width = c1 - c0
-            o = sb("o%d" % ci, [P, 4, width], F32)
+        top = sb("top", [P, 4, N], F32)
+
+        def fetch(name, h):
+            tile = sb("g_" + name, [P, 4, HALF], F32)
             for t in range(4):
-                g5 = sb("g5_%d_%d" % (ci, t), [P, width], F32)
-                g6 = sb("g6_%d_%d" % (ci, t), [P, width], F32)
-                top = sb("top%d_%d" % (ci, t), [P, width], F32)
-                nc.vector.tensor_copy(g5[:], sw[t][:].indirect(lists["n5"][:, c0 // 16 : c1 // 16]))
-                nc.vector.tensor_copy(g6[:], sw[t][:].indirect(lists["n6"][:, c0 // 16 : c1 // 16]))
-                nc.vector.tensor_tensor(top[:], g5[:], sw[t][:, c0:c1], ALU.max)
-                nc.vector.tensor_tensor(o[:, t, :], top[:], g6[:], ALU.min)
+                nc.vector.tensor_copy(tile[:, t, :], sw[t][:].indirect(lists[name][:, 16 * h : 16 * (h + 1)]))
+            return tile
+
+        def larger(g5, c0, c1):
+            nc.vector.tensor_tensor(top[:, :, c0:c1], g5[:], sp[:, :, c0:c1], ALU.max)
+
+        def smaller(g6, c0, c1):
+            o = sb("o%d" % c0, [P, 4, c1 - c0], F32)
+            nc.vector.tensor_tensor(o[:], top[:, :, c0:c1], g6, ALU.min)
             nc.sync.dma_start(out_rows[:, :, c0:c1], o[:])
-            o_in = sb("o_in%d" % ci, [P, width * 4], BF16)
-            dst = o_in[:].rearrange("p (c i t) -> p c t i", i=4, t=4)
-            src = o[:].rearrange("p t (c i) -> p c t i", i=4)
-            if ci == len(chunks) - 1:
-                nc.vector.tensor_copy(dst, src)
-            else:
-                nc.scalar.copy(dst, src)
+            return o
+
+        def regroup(copy, o, c0, c1):
+            o_in = sb("o_in%d" % c0, [P, (c1 - c0) * 4], BF16)
+            copy(o_in[:].rearrange("p (c i t) -> p c t i", i=4, t=4), o[:].rearrange("p t (c i) -> p c t i", i=4))
+            return o_in
+
+        def planes(o_in, c0, c1):
             nc.vector.quantize_mx(out=o_words[:, c0:c1].bitcast(FP8X4), scales=o_scales[:, c0:c1], in_=o_in[:])
             nc.sync.dma_start(out_words[:, c0:c1], o_words[:, c0:c1].bitcast(I32))
+
+        g5 = fetch("n5", 0)
+        g6 = fetch("n6", 0)
+        larger(g5, 0, 256)
+        g5 = fetch("n5", 1)
+        first = regroup(nc.scalar.copy, smaller(g6[:], 0, 256), 0, 256)
+        g6 = fetch("n6", 1)
+        larger(g5, 256, 512)
+        planes(first, 0, 256)
+        second = regroup(nc.scalar.copy, smaller(g6[:, :, 0:P], 256, 384), 256, 384)
+        third = regroup(nc.vector.tensor_copy, smaller(g6[:, :, P:HALF], 384, 512), 384, 512)
+        planes(second, 256, 384)
+        planes(third, 384, 512)
         scale_rows = out_2[0].bitcast(I32)
         for q in range(4):
             queue = nc.sync if q % 2 else nc.scalar

@@ -100,11 +100,11 @@ def tile_picked_twkcrossbmedminmx_none_po_kernel(
         def deal(i):
             words = sb("wd%d" % i, [P, 2 * N], U8)
             scales = sb("wds%d" % i, [P, N], U8)
-            nc.vector.tensor_copy(
+            nc.gpsimd.tensor_copy(
                 words[:].bitcast(I32).rearrange("p (t q e) -> p t q e", t=4, e=4),
                 w_raw[i][:].bitcast(I32).rearrange("p (q t e) -> p t q e", t=4, e=4),
             )
-            nc.vector.tensor_copy(
+            nc.gpsimd.tensor_copy(
                 scales[:].bitcast(I32).rearrange("p (t q e) -> p t q e", t=4, e=2),
                 w_raw_s[i][:].bitcast(I32).rearrange("p (q t e) -> p t q e", t=4, e=2),
             )
@@ -124,9 +124,9 @@ def tile_picked_twkcrossbmedminmx_none_po_kernel(
 
         pick("offs")
         deal(0)
-        pick("two", words_tag="wr0")
+        pick("two")
         deal(1)
-        pick("three", words_tag="wr1", scales_tag="wrs1")
+        pick("three")
         deal(2)
 
         ys = [sb("ys%d" % t, [P, 2 * N], F32) for t in range(4)]
@@ -221,11 +221,10 @@ def tile_picked_twkcrossbmedminmx_none_po_kernel(
 
         sw = [sb("sw%d" % t, [P, N], F32) for t in range(4)]
         sp = sb("sp", [P, 4, N], F32)
-        s_banks = [held.tile([P, N], F32, name="held%d" % t) for t in range(4)]
 
-        def score(t, c0, c1):
+        def score(acc, t, c0, c1):
             nc.tensor.matmul_mx(
-                out=s_banks[t][:, c0:c1],
+                out=acc[:],
                 lhsT=z_codes[t][0][:].bitcast(FP8X4),
                 lhsT_scale=z_codes[t][1][:],
                 rhs=z2_words[:, c0:c1].bitcast(FP8X4),
@@ -233,16 +232,16 @@ def tile_picked_twkcrossbmedminmx_none_po_kernel(
                 start=True,
                 stop=True,
             )
-            nc.scalar.activation(sw[t][:, c0:c1], s_banks[t][:, c0:c1], COPY, scale=0.0625)
+            nc.scalar.activation(sw[t][:, c0:c1], acc[:], COPY, scale=0.0625)
 
-        score(0, 0, HALF)
-        score(0, HALF, N)
+        for h in range(2):
+            score(ring.tile([P, HALF], F32, name="ring"), 0, HALF * h, HALF * (h + 1))
         for t in range(1, 4):
-            score(t, 0, N)
+            score(held.tile([P, N], F32, name="held%d" % t), t, 0, N)
         for h in range(2):
             for t in range(4):
                 cols = slice(HALF * h, HALF * (h + 1))
-                nc.scalar.activation(sp[:, t, cols], s_banks[t][:, cols], COPY, scale=0.0625)
+                nc.scalar.copy(sp[:, t, cols], sw[t][:, cols])
 
         o_words = sb("o_words", [P, N], U32)
         o_scales = sb("o_scales", [P, N], U8)

@@ -13,6 +13,7 @@ FP8X4 = mybir.dt.float8_e4m3fn_x4
 FP4X4 = mybir.dt.float4_e2m1fn_x4
 ALU = mybir.AluOpType
 COPY = mybir.ActivationFunctionType.Copy
+RELU = mybir.ActivationFunctionType.Relu
 
 P = 128
 T = 2048
@@ -198,25 +199,27 @@ def tile_picked_twkcrossbmedminmx_none_po_kernel(
 
         z2_words = sb("z2_words", [P, N], U32)
         z2_scales = sb("z2_scales", [P, N], U8)
-        z2_in = [sb("z2_in%d" % h, [P, HALF * 4], BF16) for h in range(2)]
+        pieces = ((0, 128), (128, 256), (256, 512))
+        z2_in = [sb("z2_in%d" % c0, [P, (c1 - c0) * 4], BF16) for c0, c1 in pieces]
         for c in range(2):
             cols = slice(P * c, P * (c + 1))
             flat = sb("z2_flat%d" % c, [P, 4, P], BF16)
             nc.vector.tensor_tensor(flat[:], mid[:, :, cols], hi[:, :, cols], ALU.min)
             nc.scalar.copy(
-                z2_in[0][:, N * c : N * (c + 1)].rearrange("p (c i t) -> p c t i", i=4, t=4),
+                z2_in[c][:].rearrange("p (c i t) -> p c t i", i=4, t=4),
                 flat[:].rearrange("p t (c i) -> p c t i", i=4),
             )
-        nc.vector.tensor_tensor(
-            z2_in[1][:].rearrange("p (c i t) -> p c t i", i=4, t=4),
-            mid[:, :, HALF:N].rearrange("p t (c i) -> p c t i", i=4),
-            hi[:, :, HALF:N].rearrange("p t (c i) -> p c t i", i=4),
-            ALU.min,
-        )
-        for h in range(2):
-            cols = slice(HALF * h, HALF * (h + 1))
-            nc.vector.quantize_mx(out=z2_words[:, cols].bitcast(FP8X4), scales=z2_scales[:, cols], in_=z2_in[h][:])
-        for t, tag in ((1, "z2_in0"), (2, "mid"), (3, "hi")):
+        for k in (2,):
+            c0, c1 = pieces[k]
+            nc.vector.tensor_tensor(
+                z2_in[k][:].rearrange("p (c i t) -> p c t i", i=4, t=4),
+                mid[:, :, c0:c1].rearrange("p t (c i) -> p c t i", i=4),
+                hi[:, :, c0:c1].rearrange("p t (c i) -> p c t i", i=4),
+                ALU.min,
+            )
+        for k, (c0, c1) in enumerate(pieces):
+            nc.vector.quantize_mx(out=z2_words[:, c0:c1].bitcast(FP8X4), scales=z2_scales[:, c0:c1], in_=z2_in[k][:])
+        for t, tag in ((1, "z2_in128"), (2, "mid"), (3, "hi")):
             quantize_z(t, tag)
 
         sw = [sb("sw%d" % t, [P, N], F32) for t in range(4)]
@@ -234,14 +237,12 @@ def tile_picked_twkcrossbmedminmx_none_po_kernel(
             )
             nc.scalar.activation(sw[t][:, c0:c1], acc[:], COPY, scale=0.0625)
 
-        for h in range(2):
-            score(ring.tile([P, HALF], F32, name="ring"), 0, HALF * h, HALF * (h + 1))
+        for c0, c1 in pieces:
+            score(ring.tile([P, c1 - c0], F32, name="ring"), 0, c0, c1)
+        nc.scalar.copy(sp[:, 0, 0:HALF], sw[0][:, 0:HALF])
         for t in range(1, 4):
             score(held.tile([P, N], F32, name="held%d" % t), t, 0, N)
-        for h in range(2):
-            for t in range(4):
-                cols = slice(HALF * h, HALF * (h + 1))
-                nc.scalar.copy(sp[:, t, cols], sw[t][:, cols])
+            nc.scalar.copy(sp[:, t, 0:HALF], sw[t][:, 0:HALF])
 
         o_words = sb("o_words", [P, N], U32)
         o_scales = sb("o_scales", [P, N], U8)
@@ -249,18 +250,18 @@ def tile_picked_twkcrossbmedminmx_none_po_kernel(
         out_words = out_1[0].rearrange("p n t -> p (n t)").bitcast(I32)
         top = sb("top", [P, 4, N], F32)
 
-        def fetch(name, h):
-            tile = sb("g_" + name, [P, 4, HALF], F32)
-            for t in range(4):
-                nc.vector.tensor_copy(tile[:, t, :], sw[t][:].indirect(lists[name][:, 16 * h : 16 * (h + 1)]))
-            return tile
+        def fetch(tile, name, h, rows):
+            for t in rows:
+                nc.vector.tensor_copy(tile[:, t - rows[0], :], sw[t][:].indirect(lists[name][:, 16 * h : 16 * (h + 1)]))
 
         def larger(g5, c0, c1):
             nc.vector.tensor_tensor(top[:, :, c0:c1], g5[:], sp[:, :, c0:c1], ALU.max)
 
         def smaller(g6, c0, c1):
             o = sb("o%d" % c0, [P, 4, c1 - c0], F32)
-            nc.vector.tensor_tensor(o[:], top[:, :, c0:c1], g6, ALU.min)
+            for k, part in enumerate(g6):
+                rows = slice(4 // len(g6) * k, 4 // len(g6) * (k + 1))
+                nc.vector.tensor_tensor(o[:, rows, :], top[:, rows, c0:c1], part, ALU.min)
             nc.sync.dma_start(out_rows[:, :, c0:c1], o[:])
             return o
 
@@ -271,20 +272,34 @@ def tile_picked_twkcrossbmedminmx_none_po_kernel(
 
         def planes(o_in, c0, c1):
             nc.vector.quantize_mx(out=o_words[:, c0:c1].bitcast(FP8X4), scales=o_scales[:, c0:c1], in_=o_in[:])
-            nc.sync.dma_start(out_words[:, c0:c1], o_words[:, c0:c1].bitcast(I32))
 
-        g5 = fetch("n5", 0)
-        g6 = fetch("n6", 0)
-        larger(g5, 0, 256)
-        g5 = fetch("n5", 1)
-        first = regroup(nc.scalar.copy, smaller(g6[:], 0, 256), 0, 256)
-        g6 = fetch("n6", 1)
+        excess = [sb("excess%d" % k, [P, 2, HALF], F32) for k in range(2)]
+        gain = sb("gain", [P, 4, HALF], F32)
+        for t in range(4):
+            nc.vector.tensor_tensor(
+                excess[t // 2][:, t % 2, :], sw[t][:].indirect(lists["n5"][:, 0:16]), sp[:, t, 0:HALF], ALU.subtract
+            )
+            nc.scalar.activation(gain[:, t, :], excess[t // 2][:, t % 2, :], RELU)
+        nc.gpsimd.tensor_tensor(top[:, :, 0:HALF], gain[:], sp[:, :, 0:HALF], ALU.add)
+        for t in range(4):
+            nc.scalar.copy(sp[:, t, HALF:N], sw[t][:, HALF:N])
+        g6_first = sb("g6_first", [P, 4, HALF], F32)
+        fetch(g6_first, "n6", 0, range(4))
+        g5 = sb("g5", [P, 4, HALF], F32, "excess0")
+        fetch(g5, "n5", 1, range(4))
+        g6_low = sb("g6_low", [P, 2, HALF], F32, "excess1")
+        fetch(g6_low, "n6", 1, range(0, 2))
+        first = regroup(nc.scalar.copy, smaller([g6_first[:]], 0, 256), 0, 256)
+        g6_high = sb("g6_high", [P, 2, HALF], F32, "g6_first")
+        fetch(g6_high, "n6", 1, range(2, 4))
         larger(g5, 256, 512)
         planes(first, 0, 256)
-        second = regroup(nc.scalar.copy, smaller(g6[:, :, 0:P], 256, 384), 256, 384)
-        third = regroup(nc.vector.tensor_copy, smaller(g6[:, :, P:HALF], 384, 512), 384, 512)
+        nc.sync.dma_start(out_words[:, 0:HALF], o_words[:, 0:HALF].bitcast(I32))
+        second = regroup(nc.scalar.copy, smaller([g6_low[:, :, 0:P], g6_high[:, :, 0:P]], 256, 384), 256, 384)
+        third = regroup(nc.vector.tensor_copy, smaller([g6_low[:, :, P:HALF], g6_high[:, :, P:HALF]], 384, 512), 384, 512)
         planes(second, 256, 384)
         planes(third, 384, 512)
+        nc.sync.dma_start(out_words[:, HALF:N], o_words[:, HALF:N].bitcast(I32))
         scale_rows = out_2[0].bitcast(I32)
         for q in range(4):
             queue = nc.sync if q % 2 else nc.scalar

@@ -16,10 +16,11 @@ COPY = mybir.ActivationFunctionType.Copy
 RELU = mybir.ActivationFunctionType.Relu
 
 P = 128
-T = 2048
+TOKENS = 2048
 N = 512
-HALF = 256
-FLOPS = 4 * 2 * 512 * 512 * 512
+HALF = N // 2
+TILES = 4
+FLOPS = 4 * 2 * N * N * N
 
 
 def tile_picked_twkcrossbmedminmx_none_po_kernel(
@@ -32,8 +33,14 @@ def tile_picked_twkcrossbmedminmx_none_po_kernel(
         ring = ctx.enter_context(tc.psum_pool(name="ring", bufs=4))
         held = ctx.enter_context(tc.psum_pool(name="held", bufs=1))
 
-        def sb(name, shape, dtype, tag=None):
-            return keep.tile(shape, dtype, name=name, tag=tag or name, align_bytes=64)
+        def sb(name, shape, dtype, reuse=None):
+            return keep.tile(shape, dtype, name=name, tag=reuse or name, align_bytes=64)
+
+        def interleaved(tile):
+            return tile.rearrange("p (c i t) -> p c t i", i=4, t=TILES)
+
+        def by_tiles(rows):
+            return rows.rearrange("p t (c i) -> p c t i", i=4)
 
         lists = {}
 
@@ -41,79 +48,76 @@ def tile_picked_twkcrossbmedminmx_none_po_kernel(
             lists[name] = keep.tile([P, N // 16], U16, name="list_" + name)
             nc.sync.dma_start(lists[name][:], src)
 
-        def load_scale_rows(queue, tile, src):
+        def load_scale_rows(tile, src):
             rows = src[0].bitcast(I32)
             for q in range(4):
-                queue.dma_start(tile[32 * q : 32 * q + 4, :].bitcast(I32), rows[4 * q : 4 * q + 4, :])
+                nc.sync.dma_start(tile[32 * q : 32 * q + 4, :].bitcast(I32), rows[4 * q : 4 * q + 4, :])
 
-        xs = sb("xs", [P, T], U8)
-        nc.gpsimd.memset(xs[:].bitcast(I32), 0)
-        w_raw_s = [sb("wrs%d" % i, [P, N], U8) for i in range(3)]
-        nc.gpsimd.memset(w_raw_s[0][:].bitcast(I32), 0)
-        g_rows = sb("g_rows", [P, P], F32)
-        nc.gpsimd.memset(g_rows[:], 0.0)
+        x_scale_table = sb("x_scale_table", [P, TOKENS], U8)
+        nc.gpsimd.memset(x_scale_table[:].bitcast(I32), 0)
+        w_scales_in = [sb("w_scales_in%d" % i, [P, N], U8) for i in range(3)]
+        nc.gpsimd.memset(w_scales_in[0][:].bitcast(I32), 0)
+        gain_rows = sb("gain_rows", [P, P], F32)
+        nc.gpsimd.memset(gain_rows[:], 0.0)
         for i in (1, 2):
-            nc.gpsimd.memset(w_raw_s[i][:].bitcast(I32), 0)
+            nc.gpsimd.memset(w_scales_in[i][:].bitcast(I32), 0)
         ident = sb("ident", [P, P], F32)
         make_identity(nc, ident[:])
 
-        xw = sb("xw", [P, T], I32)
-        w_raw = [sb("wr%d" % i, [P, 2 * N], U8) for i in range(3)]
+        x_word_table = sb("x_word_table", [P, TOKENS], I32)
+        w_words_in = [sb("w_words_in%d" % i, [P, 2 * N], U8) for i in range(3)]
         load_list("offs", offs)
-        load_scale_rows(nc.sync, xs, x_scales)
+        load_scale_rows(x_scale_table, x_scales)
         load_list("two", two)
-        nc.sync.dma_start(xw[:], x_words[0].rearrange("p n t -> p (n t)").bitcast(I32))
-        nc.sync.dma_start(w_raw[0][:].bitcast(I32), w1_words[0].bitcast(I32))
-        load_scale_rows(nc.sync, w_raw_s[0], w1_scales)
-        for i, g in enumerate((ga, gb)):
+        nc.sync.dma_start(x_word_table[:], x_words[0].rearrange("p n e -> p (n e)").bitcast(I32))
+        nc.sync.dma_start(w_words_in[0][:].bitcast(I32), w1_words[0].bitcast(I32))
+        load_scale_rows(w_scales_in[0], w1_scales)
+        for i, src in enumerate((ga, gb)):
             nc.sync.dma_start(
-                g_rows[4 * i : 4 * i + 4, :].rearrange("t (q r) -> t q r", r=8),
-                g.rearrange("(q t r) o -> t q (r o)", t=4, r=8),
+                gain_rows[TILES * i : TILES * (i + 1), :].rearrange("t (q r) -> t q r", r=8),
+                src.rearrange("(q t r) o -> t q (r o)", t=TILES, r=8),
             )
-        nc.sync.dma_start(w_raw[1][:].bitcast(I32), w2_words[0].bitcast(I32))
-        load_scale_rows(nc.sync, w_raw_s[1], w2_scales)
+        nc.sync.dma_start(w_words_in[1][:].bitcast(I32), w2_words[0].bitcast(I32))
+        load_scale_rows(w_scales_in[1], w2_scales)
         load_list("three", three)
         load_list("n2", n2)
         load_list("n1", n1)
-        nc.sync.dma_start(w_raw[2][:].bitcast(I32), w3_words[0].bitcast(I32))
-        load_scale_rows(nc.sync, w_raw_s[2], w3_scales)
+        nc.sync.dma_start(w_words_in[2][:].bitcast(I32), w3_words[0].bitcast(I32))
+        load_scale_rows(w_scales_in[2], w3_scales)
         for name, src in (("n3", n3), ("n4", n4), ("n5", n5), ("n6", n6)):
             load_list(name, src)
 
-        g_ps = ring.tile([P, P], F32, name="ring")
-        nc.tensor.transpose(g_ps[:], g_rows[:], ident[:])
-        gains = sb("gains", [P, 8], F32)
-        nc.scalar.activation(gains[:], g_ps[:, 0:8], COPY)
-        minus_ga = sb("minus_ga", [P, 4], F32)
-        nc.scalar.activation(minus_ga[:], g_ps[:, 0:4], COPY, scale=-1.0)
+        gain_bank = ring.tile([P, P], F32, name="ring")
+        nc.tensor.transpose(gain_bank[:], gain_rows[:], ident[:])
+        gains = sb("gains", [P, 2 * TILES], F32)
+        nc.scalar.activation(gains[:], gain_bank[:, 0 : 2 * TILES], COPY)
+        minus_ga = sb("minus_ga", [P, TILES], F32)
+        nc.scalar.activation(minus_ga[:], gain_bank[:, 0:TILES], COPY, scale=-1.0)
 
         picked = {}
 
-        def pick(name, words_tag=None, scales_tag=None):
-            words = sb("pw_" + name, [P, N], U32, words_tag)
-            scales = sb("ps_" + name, [P, N], U8, scales_tag)
-            nc.vector.tensor_copy(words[:], xw[:].bitcast(U32).indirect(lists[name][:]))
-            nc.vector.tensor_copy(scales[:], xs[:].indirect(lists[name][:]))
+        def pick(name):
+            words = sb("picked_words_" + name, [P, N], U32)
+            scales = sb("picked_scales_" + name, [P, N], U8)
+            nc.vector.tensor_copy(words[:], x_word_table[:].bitcast(U32).indirect(lists[name][:]))
+            nc.vector.tensor_copy(scales[:], x_scale_table[:].indirect(lists[name][:]))
             picked[name] = (words, scales)
 
         dealt = {}
 
         def deal(i):
-            words = sb("wd%d" % i, [P, 2 * N], U8)
-            scales = sb("wds%d" % i, [P, N], U8)
-            nc.gpsimd.tensor_copy(
-                words[:].bitcast(I32).rearrange("p (t q e) -> p t q e", t=4, e=4),
-                w_raw[i][:].bitcast(I32).rearrange("p (q t e) -> p t q e", t=4, e=4),
-            )
-            nc.gpsimd.tensor_copy(
-                scales[:].bitcast(I32).rearrange("p (t q e) -> p t q e", t=4, e=2),
-                w_raw_s[i][:].bitcast(I32).rearrange("p (q t e) -> p t q e", t=4, e=2),
-            )
+            words = sb("w_words%d" % i, [P, 2 * N], U8)
+            scales = sb("w_scales%d" % i, [P, N], U8)
+            for dst, src, run in ((words, w_words_in[i], 4), (scales, w_scales_in[i], 2)):
+                nc.gpsimd.tensor_copy(
+                    dst[:].bitcast(I32).rearrange("p (t q e) -> p t q e", t=TILES, e=run),
+                    src[:].bitcast(I32).rearrange("p (q t e) -> p t q e", t=TILES, e=run),
+                )
             dealt[i] = (words, scales)
 
-        def project(i, name, t, acc):
+        def project(i, name, t, bank):
             nc.tensor.matmul_mx(
-                out=acc[:],
+                out=bank[:],
                 lhsT=dealt[i][0][:, 2 * P * t : 2 * P * (t + 1)].bitcast(FP4X4),
                 lhsT_scale=dealt[i][1][:, P * t : P * (t + 1)],
                 rhs=picked[name][0][:].bitcast(FP8X4),
@@ -121,113 +125,111 @@ def tile_picked_twkcrossbmedminmx_none_po_kernel(
                 start=True,
                 stop=True,
             )
-            return acc
+            return bank
 
-        pick("offs")
-        deal(0)
-        pick("two")
-        deal(1)
-        pick("three")
-        deal(2)
+        for i, name in enumerate(("offs", "two", "three")):
+            pick(name)
+            deal(i)
 
-        ys = [sb("ys%d" % t, [P, 2 * N], F32) for t in range(4)]
-        dd = [sb("dd%d" % t, [P, 2 * N], F32) for t in range(4)]
-        for t in range(4):
-            acc = project(0, "offs", t, ring.tile([P, N], F32, name="ring"))
-            nc.scalar.activation(ys[t][:, 0:N], acc[:], COPY, scale=minus_ga[:, t : t + 1])
-            nc.scalar.activation(ys[t][:, N : 2 * N], acc[:], COPY, scale=gains[:, t : t + 1])
-            acc = project(1, "two", t, ring.tile([P, N], F32, name="ring"))
-            nc.scalar.activation(dd[t][:, 0:N], acc[:], COPY, scale=0.75)
-        bw = [sb("bw%d" % t, [P, 2 * N], F32) for t in range(4)]
-        bp = sb("bp", [P, 4, N], BF16)
-        for t in range(4):
-            acc = project(2, "three", t, held.tile([P, N], F32, name="held%d" % t))
-            nc.scalar.activation(bw[t][:, 0:N], acc[:], COPY, scale=gains[:, 4 + t : 5 + t])
-            nc.scalar.activation(bp[:, t, :], acc[:], COPY, scale=gains[:, 4 + t : 5 + t])
+        y_pair = [sb("y_pair%d" % t, [P, 2 * N], F32) for t in range(TILES)]
+        d_wide = [sb("d_wide%d" % t, [P, 2 * N], F32) for t in range(TILES)]
+        for t in range(TILES):
+            bank = project(0, "offs", t, ring.tile([P, N], F32, name="ring"))
+            nc.scalar.activation(y_pair[t][:, 0:N], bank[:], COPY, scale=minus_ga[:, t : t + 1])
+            nc.scalar.activation(y_pair[t][:, N : 2 * N], bank[:], COPY, scale=gains[:, t : t + 1])
+            bank = project(1, "two", t, ring.tile([P, N], F32, name="ring"))
+            nc.scalar.activation(d_wide[t][:, 0:N], bank[:], COPY, scale=0.75)
+        b_wide = [sb("b_wide%d" % t, [P, 2 * N], F32) for t in range(TILES)]
+        b_low = [sb("b_low%d" % t, [P, N], F32) for t in range(2)]
+        b_high = sb("b_high", [P, 2, N], BF16)
+        for t in range(TILES):
+            bank = project(2, "three", t, held.tile([P, N], F32, name="held%d" % t))
+            gb_t = gains[:, TILES + t : TILES + t + 1]
+            nc.scalar.activation(b_wide[t][:, 0:N], bank[:], COPY, scale=gb_t)
+            nc.scalar.activation(b_low[t][:] if t < 2 else b_high[:, t - 2, :], bank[:], COPY, scale=gb_t)
 
-        def add_turned(bank, t, first, second):
-            nc.tensor.matmul(bank[:, t, :], first, ident[:], start=True, stop=False, is_transpose=True)
-            nc.tensor.matmul(bank[:, t, :], second, ident[:], start=False, stop=True, is_transpose=True)
+        z_turned = [held.tile([P, TILES, P], F32, name="held%d" % c) for c in range(4)]
+        for t in range(TILES):
+            first = sb("z_first%d" % t, [P, N], F32)
+            second = sb("z_second%d" % t, [P, N], F32)
+            nc.vector.tensor_tensor(first[:], d_wide[t][:].indirect(lists["n2"][:]), y_pair[t][:, N : 2 * N], ALU.mult)
+            nc.vector.tensor_tensor(second[:], y_pair[t][:].indirect(lists["n1"][:]), d_wide[t][:, 0:N], ALU.mult)
+            for c in range(4):
+                cols = slice(P * c, P * (c + 1))
+                nc.tensor.matmul(z_turned[c][:, t, :], first[:, cols], ident[:], start=True, stop=False, is_transpose=True)
+                nc.tensor.matmul(z_turned[c][:, t, :], second[:, cols], ident[:], start=False, stop=True, is_transpose=True)
 
-        def round_turned(name, bank):
-            pairs = sb(name, [P, 2, P, 2], BF16)
-            nc.scalar.copy(pairs[:], bank[:].rearrange("j (u e) p -> j u p e", e=2))
-            return pairs[:].rearrange("j u p e -> j (u p e)").bitcast(F32)
+        lo = sb("lo", [P, TILES, N], BF16)
+        hi = sb("hi", [P, TILES, N], BF16)
+        above_lo = sb("above_lo", [P, TILES, N], BF16)
+        for t in range(2):
+            step = sb("step%d" % t, [P, N], F32)
+            up = sb("up%d" % t, [P, N], F32)
+            down = sb("down%d" % t, [P, N], F32)
+            nc.vector.tensor_tensor(step[:], b_wide[t][:].indirect(lists["n3"][:]), b_low[t][:], ALU.subtract)
+            nc.scalar.activation(down[:], step[:], RELU, scale=-1.0)
+            nc.scalar.activation(up[:], step[:], RELU)
+            nc.gpsimd.tensor_tensor(lo[:, t, :], b_wide[t][:, 0:N], down[:], ALU.subtract)
+            nc.gpsimd.tensor_tensor(hi[:, t, :], b_wide[t][:, 0:N], up[:], ALU.add)
 
-        z_banks = [held.tile([P, 4, P], F32, name="held%d" % b) for b in range(4)]
-        for t in range(4):
-            p1 = sb("p1_%d" % t, [P, N], F32)
-            p2 = sb("p2_%d" % t, [P, N], F32)
-            nc.vector.tensor_tensor(p1[:], dd[t][:].indirect(lists["n2"][:]), ys[t][:, N : 2 * N], ALU.mult)
-            nc.vector.tensor_tensor(p2[:], ys[t][:].indirect(lists["n1"][:]), dd[t][:, 0:N], ALU.mult)
-            for b in range(4):
-                cols = slice(P * b, P * (b + 1))
-                add_turned(z_banks[b], t, p1[:, cols], p2[:, cols])
-
-        z_in = sb("z_in", [P, N * 4], BF16)
-        z_in_words = z_in[:].bitcast(F32).rearrange("p (t m u) -> p t m u", t=4, u=2)
-        for k in range(2):
-            back = ring.tile([P, 2, 2 * P], F32, name="ring")
-            for c in range(2):
-                words = round_turned("zt%d" % (2 * k + c), z_banks[2 * k + c])
+        z_in = sb("z_in", [P, N * TILES], BF16)
+        z_in_pairs = z_in[:].bitcast(F32).rearrange("p (t m u) -> p t m u", t=TILES, u=2)
+        for h in range(2):
+            back = ring.tile([P, 2, HALF], F32, name="ring")
+            for c in (2 * h, 2 * h + 1):
+                rounded = sb("z_rounded%d" % c, [P, 2, P, 2], BF16, "step1" if c == 0 else None)
+                nc.scalar.copy(rounded[:], z_turned[c][:].rearrange("j (u e) p -> j u p e", e=2))
+                pairs = rounded[:].rearrange("j u p e -> j (u p e)").bitcast(F32)
                 for u in range(2):
-                    nc.tensor.transpose(back[:, u, P * c : P * (c + 1)], words[:, P * u : P * (u + 1)], ident[:])
-            nc.scalar.copy(z_in_words[:, :, 64 * k : 64 * (k + 1), :], back[:].rearrange("p u (m t) -> p t m u", t=4))
+                    nc.tensor.transpose(back[:, u, P * (c % 2) : P * (c % 2 + 1)], pairs[:, P * u : P * (u + 1)], ident[:])
+            nc.scalar.copy(z_in_pairs[:, :, 64 * h : 64 * (h + 1), :], back[:].rearrange("p u (m t) -> p t m u", t=TILES))
 
-        pa = sb("pa", [P, 4, N], BF16)
-        pb = sb("pb", [P, 4, N], BF16)
-        lo = sb("lo", [P, 4, N], BF16)
-        hi = sb("hi", [P, 4, N], BF16)
-        mid = sb("mid", [P, 4, N], BF16)
-        for t in range(4):
-            nc.vector.tensor_copy(pa[:, t, :], bw[t][:].indirect(lists["n3"][:]))
-            nc.vector.tensor_copy(pb[:, t, :], bw[t][:].indirect(lists["n4"][:]))
+        pb_low = sb("pb_low", [P, 2, N], BF16, "b_low1")
+        for t in range(2):
+            nc.vector.tensor_copy(pb_low[:, t, :], b_wide[t][:].indirect(lists["n4"][:]))
+        pa_high = sb("pa_high", [P, 2, N], BF16)
+        pb_high = sb("pb_high", [P, 2, N], BF16)
+        for t in range(2, TILES):
+            nc.vector.tensor_copy(pa_high[:, t - 2, :], b_wide[t][:].indirect(lists["n3"][:]))
+            nc.vector.tensor_copy(pb_high[:, t - 2, :], b_wide[t][:].indirect(lists["n4"][:]))
+        nc.vector.tensor_tensor(lo[:, 2:4, :], pa_high[:], pb_high[:], ALU.min)
+        nc.vector.tensor_tensor(hi[:, 2:4, :], pa_high[:], pb_high[:], ALU.max)
+
+        nc.vector.tensor_tensor(above_lo[:, 2:4, :], lo[:, 2:4, :], b_high[:], ALU.max)
+        nc.vector.tensor_tensor(above_lo[:, 0:2, :], lo[:, 0:2, :], pb_low[:], ALU.max)
+
         z_codes = []
 
-        def quantize_z(t, tag):
-            words = sb("z_words%d" % t, [P, P], U32, tag)
+        def quantize_z(t, reuse):
+            words = sb("z_words%d" % t, [P, P], U32, reuse)
             scales = sb("z_scales%d" % t, [P, P], U8)
             nc.vector.quantize_mx(out=words[:].bitcast(FP8X4), scales=scales[:], in_=z_in[:, N * t : N * (t + 1)])
             z_codes.append((words, scales))
 
-        quantize_z(0, None)
-        nc.vector.tensor_tensor(lo[:, 0:2, :], pa[:, 0:2, :], pb[:, 0:2, :], ALU.min)
-        nc.vector.tensor_tensor(lo[:, 2:4, :], pa[:, 2:4, :], pb[:, 2:4, :], ALU.min)
-        nc.vector.tensor_tensor(hi[:], pa[:], pb[:], ALU.max)
-        nc.vector.tensor_tensor(mid[:, 0:2, :], lo[:, 0:2, :], bp[:, 0:2, :], ALU.max)
-        nc.vector.tensor_tensor(mid[:, 2:4, :], lo[:, 2:4, :], bp[:, 2:4, :], ALU.max)
+        quantize_z(0, "lo")
 
         z2_words = sb("z2_words", [P, N], U32)
         z2_scales = sb("z2_scales", [P, N], U8)
-        pieces = ((0, 128), (128, 256), (256, 512))
-        z2_in = [sb("z2_in%d" % c0, [P, (c1 - c0) * 4], BF16) for c0, c1 in pieces]
-        for c in range(2):
-            cols = slice(P * c, P * (c + 1))
-            flat = sb("z2_flat%d" % c, [P, 4, P], BF16)
-            nc.vector.tensor_tensor(flat[:], mid[:, :, cols], hi[:, :, cols], ALU.min)
-            nc.scalar.copy(
-                z2_in[c][:].rearrange("p (c i t) -> p c t i", i=4, t=4),
-                flat[:].rearrange("p t (c i) -> p c t i", i=4),
-            )
-        for k in (2,):
-            c0, c1 = pieces[k]
-            nc.vector.tensor_tensor(
-                z2_in[k][:].rearrange("p (c i t) -> p c t i", i=4, t=4),
-                mid[:, :, c0:c1].rearrange("p t (c i) -> p c t i", i=4),
-                hi[:, :, c0:c1].rearrange("p t (c i) -> p c t i", i=4),
-                ALU.min,
-            )
-        for k, (c0, c1) in enumerate(pieces):
+        z2_pieces = ((0, P), (P, HALF), (HALF, N))
+        z2_in = [sb("z2_in%d" % c0, [P, (c1 - c0) * TILES], BF16) for c0, c1 in z2_pieces]
+        for k, (c0, c1) in enumerate(z2_pieces[:2]):
+            median = sb("median%d" % k, [P, TILES, P], BF16)
+            nc.vector.tensor_tensor(median[:], above_lo[:, :, c0:c1], hi[:, :, c0:c1], ALU.min)
+            nc.scalar.copy(interleaved(z2_in[k][:]), by_tiles(median[:]))
+        nc.vector.tensor_tensor(
+            interleaved(z2_in[2][:]), by_tiles(above_lo[:, :, HALF:N]), by_tiles(hi[:, :, HALF:N]), ALU.min
+        )
+        for k, (c0, c1) in enumerate(z2_pieces):
             nc.vector.quantize_mx(out=z2_words[:, c0:c1].bitcast(FP8X4), scales=z2_scales[:, c0:c1], in_=z2_in[k][:])
-        for t, tag in ((1, "z2_in128"), (2, "mid"), (3, "hi")):
-            quantize_z(t, tag)
+        for t, reuse in ((1, "z2_in%d" % P), (2, "above_lo"), (3, "hi")):
+            quantize_z(t, reuse)
 
-        sw = [sb("sw%d" % t, [P, N], F32) for t in range(4)]
-        sp = sb("sp", [P, 4, N], F32)
+        s_window = [sb("s_window%d" % t, [P, N], F32) for t in range(TILES)]
+        s_plain = sb("s_plain", [P, TILES, N], F32)
 
-        def score(acc, t, c0, c1):
+        def score(bank, t, c0, c1):
             nc.tensor.matmul_mx(
-                out=acc[:],
+                out=bank[:],
                 lhsT=z_codes[t][0][:].bitcast(FP8X4),
                 lhsT_scale=z_codes[t][1][:],
                 rhs=z2_words[:, c0:c1].bitcast(FP8X4),
@@ -235,72 +237,75 @@ def tile_picked_twkcrossbmedminmx_none_po_kernel(
                 start=True,
                 stop=True,
             )
-            nc.scalar.activation(sw[t][:, c0:c1], acc[:], COPY, scale=0.0625)
+            nc.scalar.activation(s_window[t][:, c0:c1], bank[:], COPY, scale=0.0625)
 
-        for c0, c1 in pieces:
+        for c0, c1 in z2_pieces:
             score(ring.tile([P, c1 - c0], F32, name="ring"), 0, c0, c1)
-        nc.scalar.copy(sp[:, 0, 0:HALF], sw[0][:, 0:HALF])
-        for t in range(1, 4):
+        nc.scalar.copy(s_plain[:, 0, 0:HALF], s_window[0][:, 0:HALF])
+        for t in range(1, TILES):
             score(held.tile([P, N], F32, name="held%d" % t), t, 0, N)
-            nc.scalar.copy(sp[:, t, 0:HALF], sw[t][:, 0:HALF])
+            nc.scalar.copy(s_plain[:, t, 0:HALF], s_window[t][:, 0:HALF])
 
-        o_words = sb("o_words", [P, N], U32)
-        o_scales = sb("o_scales", [P, N], U8)
-        out_rows = out_0.rearrange("(p t) v -> p t v", t=4)
-        out_words = out_1[0].rearrange("p n t -> p (n t)").bitcast(I32)
-        top = sb("top", [P, 4, N], F32)
+        out_words = sb("out_words", [P, N], U32)
+        out_scales = sb("out_scales", [P, N], U8)
+        out_0_rows = out_0.rearrange("(p t) v -> p t v", t=TILES)
+        out_1_words = out_1[0].rearrange("p n e -> p (n e)").bitcast(I32)
+        larger = sb("larger", [P, TILES, N], F32)
 
-        def fetch(tile, name, h, rows):
-            for t in rows:
-                nc.vector.tensor_copy(tile[:, t - rows[0], :], sw[t][:].indirect(lists[name][:, 16 * h : 16 * (h + 1)]))
+        def fetch(tile, name, h, tiles):
+            for t in tiles:
+                offsets = lists[name][:, HALF // 16 * h : HALF // 16 * (h + 1)]
+                nc.vector.tensor_copy(tile[:, t - tiles[0], :], s_window[t][:].indirect(offsets))
 
-        def larger(g5, c0, c1):
-            nc.vector.tensor_tensor(top[:, :, c0:c1], g5[:], sp[:, :, c0:c1], ALU.max)
+        def finish(parts, c0, c1):
+            result = sb("result%d" % c0, [P, TILES, c1 - c0], F32)
+            share = TILES // len(parts)
+            for k, part in enumerate(parts):
+                tiles = slice(share * k, share * (k + 1))
+                nc.vector.tensor_tensor(result[:, tiles, :], larger[:, tiles, c0:c1], part, ALU.min)
+            nc.sync.dma_start(out_0_rows[:, :, c0:c1], result[:])
+            return result
 
-        def smaller(g6, c0, c1):
-            o = sb("o%d" % c0, [P, 4, c1 - c0], F32)
-            for k, part in enumerate(g6):
-                rows = slice(4 // len(g6) * k, 4 // len(g6) * (k + 1))
-                nc.vector.tensor_tensor(o[:, rows, :], top[:, rows, c0:c1], part, ALU.min)
-            nc.sync.dma_start(out_rows[:, :, c0:c1], o[:])
-            return o
+        def round_result(copy, result, c0, c1):
+            tile = sb("out_in%d" % c0, [P, (c1 - c0) * TILES], BF16)
+            copy(interleaved(tile[:]), by_tiles(result[:]))
+            return tile
 
-        def regroup(copy, o, c0, c1):
-            o_in = sb("o_in%d" % c0, [P, (c1 - c0) * 4], BF16)
-            copy(o_in[:].rearrange("p (c i t) -> p c t i", i=4, t=4), o[:].rearrange("p t (c i) -> p c t i", i=4))
-            return o_in
-
-        def planes(o_in, c0, c1):
-            nc.vector.quantize_mx(out=o_words[:, c0:c1].bitcast(FP8X4), scales=o_scales[:, c0:c1], in_=o_in[:])
+        def quantize_out(tile, c0, c1):
+            nc.vector.quantize_mx(out=out_words[:, c0:c1].bitcast(FP8X4), scales=out_scales[:, c0:c1], in_=tile[:])
 
         excess = [sb("excess%d" % k, [P, 2, HALF], F32) for k in range(2)]
-        gain = sb("gain", [P, 4, HALF], F32)
-        for t in range(4):
-            nc.vector.tensor_tensor(
-                excess[t // 2][:, t % 2, :], sw[t][:].indirect(lists["n5"][:, 0:16]), sp[:, t, 0:HALF], ALU.subtract
-            )
-            nc.scalar.activation(gain[:, t, :], excess[t // 2][:, t % 2, :], RELU)
-        nc.gpsimd.tensor_tensor(top[:, :, 0:HALF], gain[:], sp[:, :, 0:HALF], ALU.add)
-        for t in range(4):
-            nc.scalar.copy(sp[:, t, HALF:N], sw[t][:, HALF:N])
-        g6_first = sb("g6_first", [P, 4, HALF], F32)
-        fetch(g6_first, "n6", 0, range(4))
-        g5 = sb("g5", [P, 4, HALF], F32, "excess0")
-        fetch(g5, "n5", 1, range(4))
-        g6_low = sb("g6_low", [P, 2, HALF], F32, "excess1")
-        fetch(g6_low, "n6", 1, range(0, 2))
-        first = regroup(nc.scalar.copy, smaller([g6_first[:]], 0, 256), 0, 256)
-        g6_high = sb("g6_high", [P, 2, HALF], F32, "g6_first")
-        fetch(g6_high, "n6", 1, range(2, 4))
-        larger(g5, 256, 512)
-        planes(first, 0, 256)
-        nc.sync.dma_start(out_words[:, 0:HALF], o_words[:, 0:HALF].bitcast(I32))
-        second = regroup(nc.scalar.copy, smaller([g6_low[:, :, 0:P], g6_high[:, :, 0:P]], 256, 384), 256, 384)
-        third = regroup(nc.vector.tensor_copy, smaller([g6_low[:, :, P:HALF], g6_high[:, :, P:HALF]], 384, 512), 384, 512)
-        planes(second, 256, 384)
-        planes(third, 384, 512)
-        nc.sync.dma_start(out_words[:, HALF:N], o_words[:, HALF:N].bitcast(I32))
-        scale_rows = out_2[0].bitcast(I32)
+        rise = sb("rise", [P, TILES, HALF], F32)
+        for t in range(TILES):
+            excess_t = excess[t // 2][:, t % 2, :]
+            offsets = lists["n5"][:, 0 : HALF // 16]
+            nc.vector.tensor_tensor(excess_t, s_window[t][:].indirect(offsets), s_plain[:, t, 0:HALF], ALU.subtract)
+            nc.scalar.activation(rise[:, t, :], excess_t, RELU)
+        nc.gpsimd.tensor_tensor(larger[:, :, 0:HALF], rise[:], s_plain[:, :, 0:HALF], ALU.add)
+        for t in range(TILES):
+            nc.scalar.copy(s_plain[:, t, HALF:N], s_window[t][:, HALF:N])
+        s6_first = sb("s6_first", [P, TILES, HALF], F32)
+        fetch(s6_first, "n6", 0, range(TILES))
+
+        s5_second = sb("s5_second", [P, TILES, HALF], F32, "excess0")
+        fetch(s5_second, "n5", 1, range(TILES))
+        s6_low = sb("s6_low", [P, 2, HALF], F32, "excess1")
+        fetch(s6_low, "n6", 1, range(0, 2))
+        first_in = round_result(nc.scalar.copy, finish([s6_first[:]], 0, HALF), 0, HALF)
+        s6_high = sb("s6_high", [P, 2, HALF], F32, "s6_first")
+        fetch(s6_high, "n6", 1, range(2, TILES))
+        nc.vector.tensor_tensor(larger[:, :, HALF:N], s5_second[:], s_plain[:, :, HALF:N], ALU.max)
+        quantize_out(first_in, 0, HALF)
+        nc.sync.dma_start(out_1_words[:, 0:HALF], out_words[:, 0:HALF].bitcast(I32))
+        cut = HALF + P
+        third_in = round_result(nc.scalar.copy, finish([s6_low[:, :, 0:P], s6_high[:, :, 0:P]], HALF, cut), HALF, cut)
+        last_in = round_result(
+            nc.vector.tensor_copy, finish([s6_low[:, :, P:HALF], s6_high[:, :, P:HALF]], cut, N), cut, N
+        )
+        quantize_out(third_in, HALF, cut)
+        quantize_out(last_in, cut, N)
+        nc.sync.dma_start(out_1_words[:, HALF:N], out_words[:, HALF:N].bitcast(I32))
+        out_2_rows = out_2[0].bitcast(I32)
         for q in range(4):
             queue = nc.sync if q % 2 else nc.scalar
-            queue.dma_start(scale_rows[4 * q : 4 * q + 4, :], o_scales[32 * q : 32 * q + 4, :].bitcast(I32))
+            queue.dma_start(out_2_rows[4 * q : 4 * q + 4, :], out_scales[32 * q : 32 * q + 4, :].bitcast(I32))

from contextlib import ExitStack

import concourse.mybir as mybir
from concourse.masks import make_identity

F32 = mybir.dt.float32
BF16 = mybir.dt.bfloat16
I32 = mybir.dt.int32
U32 = mybir.dt.uint32
U16 = mybir.dt.uint16
U8 = mybir.dt.uint8
FP8X4 = mybir.dt.float8_e4m3fn_x4
FP4X4 = mybir.dt.float4_e2m1fn_x4
ALU = mybir.AluOpType
COPY = mybir.ActivationFunctionType.Copy
RELU = mybir.ActivationFunctionType.Relu

P = 128
TOKENS = 2048
N = 512
HALF = N // 2
TILES = 4
FLOPS = 4 * 2 * N * N * N


def tile_picked_twkcrossbmedminmx_none_po_kernel(
    tc, x_words, x_scales, w1_words, w1_scales, w2_words, w2_scales, w3_words, w3_scales,
    ga, gb, offs, two, n1, n2, three, n3, n4, n5, n6, out_0, out_1, out_2,
):
    nc = tc.nc
    with ExitStack() as ctx:
        keep = ctx.enter_context(tc.tile_pool(name="keep", bufs=1))
        ring = ctx.enter_context(tc.psum_pool(name="ring", bufs=4))
        held = ctx.enter_context(tc.psum_pool(name="held", bufs=1))

        def sb(name, shape, dtype, reuse=None):
            return keep.tile(shape, dtype, name=name, tag=reuse or name, align_bytes=64)

        def interleaved(tile):
            return tile.rearrange("p (c i t) -> p c t i", i=4, t=TILES)

        def by_tiles(rows):
            return rows.rearrange("p t (c i) -> p c t i", i=4)

        lists = {}

        def load_list(name, src):
            lists[name] = keep.tile([P, N // 16], U16, name="list_" + name)
            nc.sync.dma_start(lists[name][:], src)

        def load_scale_rows(tile, src):
            rows = src[0].bitcast(I32)
            for q in range(4):
                nc.sync.dma_start(tile[32 * q : 32 * q + 4, :].bitcast(I32), rows[4 * q : 4 * q + 4, :])

        x_scale_table = sb("x_scale_table", [P, TOKENS], U8)
        nc.gpsimd.memset(x_scale_table[:].bitcast(I32), 0)
        w_scales_in = [sb("w_scales_in%d" % i, [P, N], U8) for i in range(3)]
        nc.gpsimd.memset(w_scales_in[0][:].bitcast(I32), 0)
        gain_rows = sb("gain_rows", [P, P], F32)
        nc.gpsimd.memset(gain_rows[:], 0.0)
        for i in (1, 2):
            nc.gpsimd.memset(w_scales_in[i][:].bitcast(I32), 0)
        ident = sb("ident", [P, P], F32)
        make_identity(nc, ident[:])

        x_word_table = sb("x_word_table", [P, TOKENS], I32)
        w_words_in = [sb("w_words_in%d" % i, [P, 2 * N], U8) for i in range(3)]
        load_list("offs", offs)
        load_scale_rows(x_scale_table, x_scales)
        load_list("two", two)
        nc.sync.dma_start(x_word_table[:], x_words[0].rearrange("p n e -> p (n e)").bitcast(I32))
        nc.sync.dma_start(w_words_in[0][:].bitcast(I32), w1_words[0].bitcast(I32))
        load_scale_rows(w_scales_in[0], w1_scales)
        for i, src in enumerate((ga, gb)):
            nc.sync.dma_start(
                gain_rows[TILES * i : TILES * (i + 1), :].rearrange("t (q r) -> t q r", r=8),
                src.rearrange("(q t r) o -> t q (r o)", t=TILES, r=8),
            )
        nc.sync.dma_start(w_words_in[1][:].bitcast(I32), w2_words[0].bitcast(I32))
        load_scale_rows(w_scales_in[1], w2_scales)
        load_list("three", three)
        load_list("n2", n2)
        load_list("n1", n1)
        nc.sync.dma_start(w_words_in[2][:].bitcast(I32), w3_words[0].bitcast(I32))
        load_scale_rows(w_scales_in[2], w3_scales)
        for name, src in (("n3", n3), ("n4", n4), ("n5", n5), ("n6", n6)):
            load_list(name, src)

        gain_bank = ring.tile([P, P], F32, name="ring")
        nc.tensor.transpose(gain_bank[:], gain_rows[:], ident[:])
        gains = sb("gains", [P, 2 * TILES], F32)
        nc.scalar.activation(gains[:], gain_bank[:, 0 : 2 * TILES], COPY)
        minus_ga = sb("minus_ga", [P, TILES], F32)
        nc.scalar.activation(minus_ga[:], gain_bank[:, 0:TILES], COPY, scale=-1.0)

        picked = {}

        def pick(name):
            words = sb("picked_words_" + name, [P, N], U32)
            scales = sb("picked_scales_" + name, [P, N], U8)
            nc.vector.tensor_copy(words[:], x_word_table[:].bitcast(U32).indirect(lists[name][:]))
            nc.vector.tensor_copy(scales[:], x_scale_table[:].indirect(lists[name][:]))
            picked[name] = (words, scales)

        dealt = {}

        def deal(i):
            words = sb("w_words%d" % i, [P, 2 * N], U8)
            scales = sb("w_scales%d" % i, [P, N], U8)
            for dst, src, run in ((words, w_words_in[i], 4), (scales, w_scales_in[i], 2)):
                nc.gpsimd.tensor_copy(
                    dst[:].bitcast(I32).rearrange("p (t q e) -> p t q e", t=TILES, e=run),
                    src[:].bitcast(I32).rearrange("p (q t e) -> p t q e", t=TILES, e=run),
                )
            dealt[i] = (words, scales)

        def project(i, name, t, bank):
            nc.tensor.matmul_mx(
                out=bank[:],
                lhsT=dealt[i][0][:, 2 * P * t : 2 * P * (t + 1)].bitcast(FP4X4),
                lhsT_scale=dealt[i][1][:, P * t : P * (t + 1)],
                rhs=picked[name][0][:].bitcast(FP8X4),
                rhs_scale=picked[name][1][:],
                start=True,
                stop=True,
            )
            return bank

        for i, name in enumerate(("offs", "two", "three")):
            pick(name)
            deal(i)

        y_pair = [sb("y_pair%d" % t, [P, 2 * N], F32) for t in range(TILES)]
        d_wide = [sb("d_wide%d" % t, [P, 2 * N], F32) for t in range(TILES)]
        for t in range(TILES):
            bank = project(0, "offs", t, ring.tile([P, N], F32, name="ring"))
            nc.scalar.activation(y_pair[t][:, 0:N], bank[:], COPY, scale=minus_ga[:, t : t + 1])
            nc.scalar.activation(y_pair[t][:, N : 2 * N], bank[:], COPY, scale=gains[:, t : t + 1])
            bank = project(1, "two", t, ring.tile([P, N], F32, name="ring"))
            nc.scalar.activation(d_wide[t][:, 0:N], bank[:], COPY, scale=0.75)
        b_wide = [sb("b_wide%d" % t, [P, 2 * N], F32) for t in range(TILES)]
        b_low = [sb("b_low%d" % t, [P, N], F32) for t in range(2)]
        b_high = sb("b_high", [P, 2, N], BF16)
        for t in range(TILES):
            bank = project(2, "three", t, held.tile([P, N], F32, name="held%d" % t))
            gb_t = gains[:, TILES + t : TILES + t + 1]
            nc.scalar.activation(b_wide[t][:, 0:N], bank[:], COPY, scale=gb_t)
            nc.scalar.activation(b_low[t][:] if t < 2 else b_high[:, t - 2, :], bank[:], COPY, scale=gb_t)

        z_turned = [held.tile([P, TILES, P], F32, name="held%d" % c) for c in range(4)]
        for t in range(TILES):
            first = sb("z_first%d" % t, [P, N], F32)
            second = sb("z_second%d" % t, [P, N], F32)
            nc.vector.tensor_tensor(first[:], d_wide[t][:].indirect(lists["n2"][:]), y_pair[t][:, N : 2 * N], ALU.mult)
            nc.vector.tensor_tensor(second[:], y_pair[t][:].indirect(lists["n1"][:]), d_wide[t][:, 0:N], ALU.mult)
            for c in range(4):
                cols = slice(P * c, P * (c + 1))
                nc.tensor.matmul(z_turned[c][:, t, :], first[:, cols], ident[:], start=True, stop=False, is_transpose=True)
                nc.tensor.matmul(z_turned[c][:, t, :], second[:, cols], ident[:], start=False, stop=True, is_transpose=True)

        lo = sb("lo", [P, TILES, N], BF16)
        hi = sb("hi", [P, TILES, N], BF16)
        above_lo = sb("above_lo", [P, TILES, N], BF16)
        for t in range(2):
            step = sb("step%d" % t, [P, N], F32)
            up = sb("up%d" % t, [P, N], F32)
            down = sb("down%d" % t, [P, N], F32)
            nc.vector.tensor_tensor(step[:], b_wide[t][:].indirect(lists["n3"][:]), b_low[t][:], ALU.subtract)
            nc.scalar.activation(down[:], step[:], RELU, scale=-1.0)
            nc.scalar.activation(up[:], step[:], RELU)
            nc.gpsimd.tensor_tensor(lo[:, t, :], b_wide[t][:, 0:N], down[:], ALU.subtract)
            nc.gpsimd.tensor_tensor(hi[:, t, :], b_wide[t][:, 0:N], up[:], ALU.add)

        z_in = sb("z_in", [P, N * TILES], BF16)
        z_in_pairs = z_in[:].bitcast(F32).rearrange("p (t m u) -> p t m u", t=TILES, u=2)
        for h in range(2):
            back = ring.tile([P, 2, HALF], F32, name="ring")
            for c in (2 * h, 2 * h + 1):
                rounded = sb("z_rounded%d" % c, [P, 2, P, 2], BF16, "step1" if c == 0 else None)
                nc.scalar.copy(rounded[:], z_turned[c][:].rearrange("j (u e) p -> j u p e", e=2))
                pairs = rounded[:].rearrange("j u p e -> j (u p e)").bitcast(F32)
                for u in range(2):
                    nc.tensor.transpose(back[:, u, P * (c % 2) : P * (c % 2 + 1)], pairs[:, P * u : P * (u + 1)], ident[:])
            nc.scalar.copy(z_in_pairs[:, :, 64 * h : 64 * (h + 1), :], back[:].rearrange("p u (m t) -> p t m u", t=TILES))

        pb_low = sb("pb_low", [P, 2, N], BF16, "b_low1")
        for t in range(2):
            nc.vector.tensor_copy(pb_low[:, t, :], b_wide[t][:].indirect(lists["n4"][:]))
        pa_high = sb("pa_high", [P, 2, N], BF16)
        pb_high = sb("pb_high", [P, 2, N], BF16)
        for t in range(2, TILES):
            nc.vector.tensor_copy(pa_high[:, t - 2, :], b_wide[t][:].indirect(lists["n3"][:]))
            nc.vector.tensor_copy(pb_high[:, t - 2, :], b_wide[t][:].indirect(lists["n4"][:]))
        nc.vector.tensor_tensor(lo[:, 2:4, :], pa_high[:], pb_high[:], ALU.min)
        nc.vector.tensor_tensor(hi[:, 2:4, :], pa_high[:], pb_high[:], ALU.max)

        nc.vector.tensor_tensor(above_lo[:, 2:4, :], lo[:, 2:4, :], b_high[:], ALU.max)
        nc.vector.tensor_tensor(above_lo[:, 0:2, :], lo[:, 0:2, :], pb_low[:], ALU.max)

        z_codes = []

        def quantize_z(t, reuse):
            words = sb("z_words%d" % t, [P, P], U32, reuse)
            scales = sb("z_scales%d" % t, [P, P], U8)
            nc.vector.quantize_mx(out=words[:].bitcast(FP8X4), scales=scales[:], in_=z_in[:, N * t : N * (t + 1)])
            z_codes.append((words, scales))

        quantize_z(0, "lo")

        z2_words = sb("z2_words", [P, N], U32)
        z2_scales = sb("z2_scales", [P, N], U8)
        z2_pieces = ((0, P), (P, HALF), (HALF, N))
        z2_in = [sb("z2_in%d" % c0, [P, (c1 - c0) * TILES], BF16) for c0, c1 in z2_pieces]
        for k, (c0, c1) in enumerate(z2_pieces[:2]):
            median = sb("median%d" % k, [P, TILES, P], BF16)
            nc.vector.tensor_tensor(median[:], above_lo[:, :, c0:c1], hi[:, :, c0:c1], ALU.min)
            nc.scalar.copy(interleaved(z2_in[k][:]), by_tiles(median[:]))
        nc.vector.tensor_tensor(
            interleaved(z2_in[2][:]), by_tiles(above_lo[:, :, HALF:N]), by_tiles(hi[:, :, HALF:N]), ALU.min
        )
        for k, (c0, c1) in enumerate(z2_pieces):
            nc.vector.quantize_mx(out=z2_words[:, c0:c1].bitcast(FP8X4), scales=z2_scales[:, c0:c1], in_=z2_in[k][:])
        for t, reuse in ((1, "z2_in%d" % P), (2, "above_lo"), (3, "hi")):
            quantize_z(t, reuse)

        s_window = [sb("s_window%d" % t, [P, N], F32) for t in range(TILES)]
        s_plain = sb("s_plain", [P, TILES, N], F32)

        def score(bank, t, c0, c1):
            nc.tensor.matmul_mx(
                out=bank[:],
                lhsT=z_codes[t][0][:].bitcast(FP8X4),
                lhsT_scale=z_codes[t][1][:],
                rhs=z2_words[:, c0:c1].bitcast(FP8X4),
                rhs_scale=z2_scales[:, c0:c1],
                start=True,
                stop=True,
            )
            nc.scalar.activation(s_window[t][:, c0:c1], bank[:], COPY, scale=0.0625)

        for c0, c1 in z2_pieces:
            score(ring.tile([P, c1 - c0], F32, name="ring"), 0, c0, c1)
        nc.scalar.copy(s_plain[:, 0, 0:HALF], s_window[0][:, 0:HALF])
        for t in range(1, TILES):
            score(held.tile([P, N], F32, name="held%d" % t), t, 0, N)
            nc.scalar.copy(s_plain[:, t, 0:HALF], s_window[t][:, 0:HALF])

        out_words = sb("out_words", [P, N], U32)
        out_scales = sb("out_scales", [P, N], U8)
        out_0_rows = out_0.rearrange("(p t) v -> p t v", t=TILES)
        out_1_words = out_1[0].rearrange("p n e -> p (n e)").bitcast(I32)
        larger = sb("larger", [P, TILES, N], F32)

        def fetch(tile, name, h, tiles):
            for t in tiles:
                offsets = lists[name][:, HALF // 16 * h : HALF // 16 * (h + 1)]
                nc.vector.tensor_copy(tile[:, t - tiles[0], :], s_window[t][:].indirect(offsets))

        def finish(parts, c0, c1):
            result = sb("result%d" % c0, [P, TILES, c1 - c0], F32)
            share = TILES // len(parts)
            for k, part in enumerate(parts):
                tiles = slice(share * k, share * (k + 1))
                nc.vector.tensor_tensor(result[:, tiles, :], larger[:, tiles, c0:c1], part, ALU.min)
            nc.sync.dma_start(out_0_rows[:, :, c0:c1], result[:])
            return result

        def round_result(copy, result, c0, c1):
            tile = sb("out_in%d" % c0, [P, (c1 - c0) * TILES], BF16)
            copy(interleaved(tile[:]), by_tiles(result[:]))
            return tile

        def quantize_out(tile, c0, c1):
            nc.vector.quantize_mx(out=out_words[:, c0:c1].bitcast(FP8X4), scales=out_scales[:, c0:c1], in_=tile[:])

        excess = [sb("excess%d" % k, [P, 2, HALF], F32) for k in range(2)]
        rise = sb("rise", [P, TILES, HALF], F32)
        for t in range(TILES):
            excess_t = excess[t // 2][:, t % 2, :]
            offsets = lists["n5"][:, 0 : HALF // 16]
            nc.vector.tensor_tensor(excess_t, s_window[t][:].indirect(offsets), s_plain[:, t, 0:HALF], ALU.subtract)
            nc.scalar.activation(rise[:, t, :], excess_t, RELU)
        nc.gpsimd.tensor_tensor(larger[:, :, 0:HALF], rise[:], s_plain[:, :, 0:HALF], ALU.add)
        for t in range(TILES):
            nc.scalar.copy(s_plain[:, t, HALF:N], s_window[t][:, HALF:N])
        s6_first = sb("s6_first", [P, TILES, HALF], F32)
        fetch(s6_first, "n6", 0, range(TILES))

        s5_second = sb("s5_second", [P, TILES, HALF], F32, "excess0")
        fetch(s5_second, "n5", 1, range(TILES))
        s6_low = sb("s6_low", [P, 2, HALF], F32, "excess1")
        fetch(s6_low, "n6", 1, range(0, 2))
        first_in = round_result(nc.scalar.copy, finish([s6_first[:]], 0, HALF), 0, HALF)
        s6_high = sb("s6_high", [P, 2, HALF], F32, "s6_first")
        fetch(s6_high, "n6", 1, range(2, TILES))
        nc.vector.tensor_tensor(larger[:, :, HALF:N], s5_second[:], s_plain[:, :, HALF:N], ALU.max)
        quantize_out(first_in, 0, HALF)
        nc.sync.dma_start(out_1_words[:, 0:HALF], out_words[:, 0:HALF].bitcast(I32))
        cut = HALF + P
        third_in = round_result(nc.scalar.copy, finish([s6_low[:, :, 0:P], s6_high[:, :, 0:P]], HALF, cut), HALF, cut)
        last_in = round_result(
            nc.vector.tensor_copy, finish([s6_low[:, :, P:HALF], s6_high[:, :, P:HALF]], cut, N), cut, N
        )
        quantize_out(third_in, HALF, cut)
        quantize_out(last_in, cut, N)
        nc.sync.dma_start(out_1_words[:, HALF:N], out_words[:, HALF:N].bitcast(I32))
        out_2_rows = out_2[0].bitcast(I32)
        for q in range(4):
            queue = nc.sync if q % 2 else nc.scalar
            queue.dma_start(out_2_rows[4 * q : 4 * q + 4, :], out_scales[32 * q : 32 * q + 4, :].bitcast(I32))
